import numpy as np
import ml_dtypes


def mxq(x, axis, fmt="e4m3"):
    dtype, down = {"e4m3": (ml_dtypes.float8_e4m3fn, 7), "e5m2": (ml_dtypes.float8_e5m2, 14)}[fmt]
    v = np.moveaxis(np.asarray(x, np.float32).astype(ml_dtypes.bfloat16).astype(np.float64), axis, -1)
    blocks = v.reshape(v.shape[:-1] + (-1, 32))
    amax = np.abs(blocks).max(-1, keepdims=True)
    byte = np.maximum(np.where(amax > 0, np.frexp(amax)[1] - 1 + 127, 0) - down, 1)
    scale = np.exp2(byte - 127.0)
    codes = (blocks / scale).astype(np.float32).astype(dtype).astype(np.float64)
    return np.moveaxis((codes * scale).reshape(v.shape), -1, axis)


WIDE = False


def mx_kscale(k):
    if not WIDE:
        return np.ones(k)
    levels = np.array([10, -10, 5, -5, 0])
    if k % 512:
        return np.exp2(np.random.permutation(np.resize(levels, k // 32))).repeat(32)
    a = np.empty((k // 512, 16))
    for p in range(k // 512):
        a[p, :8] = np.random.permutation(np.resize(levels, 8))
        for g in range(8):
            far = levels[np.abs(levels - a[p, g]) >= 10]
            a[p, g + 8] = far[np.random.randint(len(far))]
    return np.exp2(a.ravel()).repeat(32)


BF16 = ml_dtypes.bfloat16


def bf(x):
    return np.asarray(x, np.float32).astype(BF16)


def f64(x):
    return np.asarray(x).astype(np.float64)


E2M1 = np.array([0.0, 0.5, 1.0, 1.5, 2.0, 3.0, 4.0, 6.0, -0.0, -0.5, -1.0, -1.5, -2.0, -3.0, -4.0, -6.0])


def pack_weight(w, fmt):
    k, n = w.shape
    w = f64(bf(w)).reshape(k // 32, 32, n)
    amax = np.abs(w).max(1)
    if fmt == "e4m3":
        byte = np.frexp(amax)[1] - 1 + 127 - 7
    else:
        mant, ex = np.frexp(amax / 6.0)
        byte = np.where(mant > 0.5, ex, ex - 1) + 127
    byte = np.clip(np.where(amax > 0, byte, 1), 1, 254)
    scaled = (w * np.exp2(127.0 - byte)[:, None, :]).reshape(k, n).astype(np.float32)
    by_word = np.ascontiguousarray(scaled.reshape(k // 512, 128, 4, n).transpose(0, 1, 3, 2))
    if fmt == "e4m3":
        words = by_word.astype(ml_dtypes.float8_e4m3fn).view(np.uint8)
    else:
        c = by_word.astype(ml_dtypes.float4_e2m1fn).view(np.uint8) & 0xF
        words = c[..., 0::2] | (c[..., 1::2] << 4)
    return np.ascontiguousarray(words), np.ascontiguousarray(byte.astype(np.uint8).reshape(k // 512, 16, n))


def unpack_weight(words, scales, fmt):
    g, p, n, _ = words.shape
    if fmt == "e4m3":
        vals = np.ascontiguousarray(words).view(ml_dtypes.float8_e4m3fn).astype(np.float64)
    else:
        nib = np.empty((g, p, n, 4), np.uint8)
        nib[..., 0::2] = words & 0xF
        nib[..., 1::2] = words >> 4
        vals = E2M1[nib]
    vals = vals * np.repeat(np.exp2(scales.astype(np.float64) - 127.0), 8, axis=1)[..., None]
    return vals.transpose(0, 1, 3, 2).reshape(g * 512, n)
def pack4(w):
    words, scales = pack_weight(w, "e2m1")
    return words.reshape(words.shape[0], 128, -1), scales


def unpack4(words, scales):
    return unpack_weight(words.reshape(words.shape[0], 128, -1, 2), scales, "e2m1")


M, L, N, C, P, D = 2048, 1024, 1024, 512, 64, 2


def setup_inputs():
    s, t = mx_kscale(L), mx_kscale(N)
    w1 = np.random.standard_normal((L, N)) / np.sqrt(L) / s[:, None] * t
    w2 = 2.5 * np.random.standard_normal((N, C)) / np.sqrt(N) / t[:, None]
    w1_words, w1_scales = pack4(w1)
    w2_words, w2_scales = pack_weight(w2, "e4m3")
    return {"mip0": bf(np.random.standard_normal((M, L)) * s),
            "mip1": bf(np.random.standard_normal((M, L)) * s),
            "frac": bf(np.random.uniform(0.0, 1.0, M)),
            "uv": bf(np.random.uniform(-1.0, 1.0, (M, D))),
            "w1_words": w1_words, "w1_scales": w1_scales,
            "b1": bf(0.3 * np.random.standard_normal(N) * t),
            "omega": bf(np.random.uniform(-1.2, 1.2, (D, N))),
            "phi": bf(np.random.uniform(-0.7, 0.7, N)),
            "mu": bf(np.random.uniform(-1.0, 1.0, (D, N))),
            "gamma": bf(np.random.uniform(0.3, 1.0, N)),
            "w2_words": w2_words, "w2_scales": w2_scales,
            "b2": bf(0.3 * np.random.standard_normal(C))}


def gabor(uv, omega, phi, mu, gamma):
    u, v = uv[:, 0:1], uv[:, 1:2]
    wave = np.sin(u * omega[0] + v * omega[1] + phi)
    dist2 = (u - mu[0]) ** 2 + (v - mu[1]) ** 2
    return wave * np.exp(-0.5 * gamma * dist2)


def reference(mip0, mip1, frac, uv, w1_words, w1_scales, b1, omega, phi, mu, gamma, w2_words, w2_scales, b2):
    f = f64(frac)[:, None]
    z = (1.0 - f) * f64(mip0) + f * f64(mip1)
    a = mxq(z, 1, "e4m3") @ unpack4(w1_words, w1_scales)
    h = (a + f64(b1)) * gabor(f64(uv), f64(omega), f64(phi), f64(mu), f64(gamma))
    y = (mxq(h, 1, "e4m3") @ unpack_weight(w2_words, w2_scales, "e4m3")) + f64(b2)
    nx, ny = y[:, :P], y[:, P:2 * P]
    r = 1.0 / np.sqrt(1.0 + nx * nx + ny * ny)
    normal = np.concatenate([nx * r, ny * r], axis=1)
    maps = np.tanh(y[:, 2 * P:])
    return normal, maps

@@ -1,0 +1,513 @@
+from contextlib import ExitStack
+
+import concourse.mybir as mybir
+from concourse.masks import make_identity
+
+M, L, N, C, PL = 2048, 1024, 1024, 512, 64
+FLOPS = 2 * M * L * N + 2 * M * N * C
+
+F32 = mybir.dt.float32
+BF16 = mybir.dt.bfloat16
+U32 = mybir.dt.uint32
+I32 = mybir.dt.int32
+U8 = mybir.dt.uint8
+FP8X4 = mybir.dt.float8_e4m3fn_x4
+FP4X4 = mybir.dt.float4_e2m1fn_x4
+ALU = mybir.AluOpType
+ACT = mybir.ActivationFunctionType
+
+P = 128
+TILES = 16
+CHUNKS = 4
+TPC = 4
+CH = 512
+G = 2
+T = 4
+JT = 8
+PE_ARG = 6
+EV_HEAD = "VVVVVVVV"
+PE_FIRST = 8
+ARGB = 5
+ZP1 = 7
+TB1 = "S"
+EARLY = True
+W1_ENG = "V"
+
+
+def tile_gabor_texture_decoder_f7_kernel(
+    tc, mip0, mip1, frac, uv, w1_words, w1_scales, b1, omega, phi, mu, gamma, w2_words, w2_scales, b2, out_0, out_1
+):
+    nc = tc.nc
+    mip_v = [m.rearrange("(p n) l -> p n l", n=TILES) for m in (mip0, mip1)]
+    out0_v = out_0.rearrange("(p n) c -> p n c", n=TILES)
+    out1_v = out_1.rearrange("(p n) c -> p n c", n=TILES)
+
+    with ExitStack() as ctx:
+        keep = ctx.enter_context(tc.tile_pool(name="keep", bufs=1))
+        work = ctx.enter_context(tc.tile_pool(name="work", bufs=2))
+        psum = ctx.enter_context(tc.psum_pool(name="psum", bufs=4))
+        ctx.enter_context(tc.manual_schedule())
+
+        def const(name, shape, dtype):
+            return keep.tile(shape, dtype, name=name, align_bytes=64)
+
+        def bank(tag, shape, dtype):
+            return psum.tile(shape, dtype, name=tag, tag=tag)
+
+        s1_raw = work.tile([P, G, N], U8, name="s1_raw", tag="window", align_bytes=64)
+        om_rows = const("om_rows", [P, N], BF16)
+        mu_rows = const("mu_rows", [P, N], BF16)
+        feat_t = work.tile([P, TILES, P], BF16, name="feat_t", tag="hin", align_bytes=64)
+        s2 = const("s2", [P, G, C], U8)
+        nc.vector.memset(om_rows[:].bitcast(I32), 0)
+        nc.vector.memset(s1_raw[:].bitcast(I32), 0)
+        nc.vector.memset(feat_t[:].bitcast(I32), 0)
+        nc.vector.memset(mu_rows[:].bitcast(I32), 0)
+        nc.vector.memset(mu_rows[0:6, :], -0.5)
+        nc.vector.memset(s2[:].bitcast(I32), 0)
+        ident = const("ident", [P, P], F32)
+        make_identity(nc, ident[:])
+
+        uv_sb = const("uv_sb", [P, TILES * 2], BF16)
+        nc.sync.dma_start(out=uv_sb[:], in_=uv.rearrange("(p n) d -> p (n d)", n=TILES))
+        om_j = const("om_j", [P, 2 * G, T], BF16)
+        nc.scalar.dma_start(out=om_j[:], in_=omega.rearrange("d (g p t) -> p (d g) t", p=P, t=T))
+        phi_j = const("phi_j", [P, G, T], BF16)
+        nc.scalar.dma_start(out=phi_j[:], in_=phi.rearrange("(g p t) -> p g t", p=P, t=T))
+        nc.sync.dma_start(out=om_rows[0:2, :], in_=omega)
+        frac_sb = const("frac_sb", [P, TILES], BF16)
+        nc.sync.dma_start(out=frac_sb[:], in_=frac.rearrange("(p n) -> p n", n=TILES))
+        w1_raw = work.tile([P, G, 2 * N], U8, name="w1_raw", tag="window", align_bytes=64)
+        nc.sync.dma_start(out=w1_raw[:].bitcast(I32), in_=w1_words.rearrange("g p b -> p g b").bitcast(I32))
+        for q in range(4):
+            nc.sync.dma_start(
+                out=s1_raw[32 * q : 32 * q + 4, :, :].bitcast(I32),
+                in_=w1_scales[:, 4 * q : 4 * q + 4, :].rearrange("g r n -> r g n").bitcast(I32),
+            )
+
+        mips = {}
+
+        def load_mips(k):
+            for level in range(2):
+                m = work.tile([P, 2, L], BF16, name="mip%d" % level, tag="mip%d" % level, bufs=4)
+                nc.sync.dma_start(out=m[:], in_=mip_v[level][:, 2 * k : 2 * (k + 1), :])
+                mips[k, level] = m
+
+        load_mips(0)
+        mu_j = const("mu_j", [P, 2 * G, T], BF16)
+        nc.sync.dma_start(out=mu_j[:], in_=mu.rearrange("d (g p t) -> p (d g) t", p=P, t=T))
+        gam_j = const("gam_j", [P, G, T], BF16)
+        nc.sync.dma_start(out=gam_j[:], in_=gamma.rearrange("(g p t) -> p g t", p=P, t=T))
+        b1_j = const("b1_j", [P, G, T], BF16)
+        nc.sync.dma_start(out=b1_j[:], in_=b1.rearrange("(g p t) -> p g t", p=P, t=T))
+        load_mips(1)
+        nc.sync.dma_start(out=mu_rows[0:2, :], in_=mu)
+        load_mips(2)
+        load_mips(3)
+        w2 = const("w2", [P, G, C], U32)
+        nc.sync.dma_start(out=w2[:].bitcast(I32), in_=w2_words.rearrange("g p n t -> p g (n t)").bitcast(I32))
+        for q in range(4):
+            nc.sync.dma_start(
+                out=s2[32 * q : 32 * q + 4, :, :].bitcast(I32),
+                in_=w2_scales[:, 4 * q : 4 * q + 4, :].rearrange("g r n -> r g n").bitcast(I32),
+            )
+        b2_bc = const("b2_bc", [P, C], BF16)
+        nc.sync.dma_start(out=b2_bc[:], in_=b2.partition_broadcast(P))
+
+        warm = const("warm", [P, 1], F32)
+        nc.scalar.activation(out=warm[:], in_=ident[:, 0:1], func=ACT.Sin)
+        ident_b = const("ident_b", [P, P], BF16)
+        nc.vector.tensor_copy(out=ident_b[:], in_=ident[:])
+
+        uv_f = const("uv_f", [P, TILES * 2], F32)
+        uv3 = uv_sb[:].rearrange("p (n d) -> p n d", d=2)
+        uv_sq = const("uv_sq", [P, TILES, 2], F32)
+        om_f = om_j[:].rearrange("p a t -> p (a t)")
+        om_sq = const("om_sq", [P, JT], F32)
+        om_fix = const("om_fix", [P, JT], F32)
+        om0 = const("om0", [P, JT], F32)
+        om_inv = const("om_inv", [P, JT], F32)
+        ratio = const("ratio", [P, JT], F32)
+        phi_f = const("phi_f", [P, JT], F32)
+        frac_f = const("frac_f", [P, TILES], F32)
+        nc.vector.tensor_copy(out=uv_f[:], in_=uv_sb[:])
+        nc.vector.tensor_tensor(out=uv_sq[:], in0=uv3, in1=uv3, op=ALU.mult)
+        nc.vector.tensor_tensor(out=om_sq[:], in0=om_f[:, 0:JT], in1=om_f[:, 0:JT], op=ALU.mult)
+        nc.vector.tensor_copy(out=feat_t[:, :, 0:2], in_=uv3)
+        nc.vector.tensor_scalar(out=om_fix[:], in0=om_sq[:], scalar1=2.0**-80, scalar2=2.0**-39, op0=ALU.is_lt, op1=ALU.mult)
+        nc.vector.tensor_copy(out=feat_t[:, :, 2:4], in_=uv_sq[:])
+        nc.vector.tensor_tensor(out=om0[:], in0=om_f[:, 0:JT], in1=om_fix[:], op=ALU.add)
+        nc.vector.tensor_tensor(out=feat_t[:, :, 4:6], in0=uv_sq[:], in1=feat_t[:, :, 2:4], op=ALU.subtract)
+        nc.vector.reciprocal(out=om_inv[:], in_=om0[:])
+        nc.vector.tensor_copy(out=phi_f[:], in_=phi_j[:].rearrange("p g t -> p (g t)"))
+        nc.vector.tensor_tensor(out=ratio[:], in0=om_f[:, JT : 2 * JT], in1=om_inv[:], op=ALU.mult)
+
+        one_minus = {}
+
+        def make_one_minus(c):
+            o = const("one_minus%d" % c, [P, 2], F32)
+            nc.vector.tensor_scalar(
+                out=o[:], in0=frac_f[:, 2 * c : 2 * (c + 1)], scalar1=-1.0, scalar2=1.0, op0=ALU.mult, op1=ALU.add
+            )
+            one_minus[c] = o
+
+        def make_fractions():
+            nc.vector.tensor_copy(out=frac_f[:], in_=frac_sb[:])
+            make_one_minus(0)
+
+        u_bank, v_rows, wave, feat = {}, {}, {}, {}
+
+        def spread(c, d, tag):
+            b = bank(tag, [P, CH], F32)
+            for n in range(TPC):
+                col = 2 * (TPC * c + n) + d
+                nc.tensor.transpose(b[:, P * n : P * (n + 1)], uv_f[:, col : col + 1].to_broadcast([P, P]), ident[:])
+            return b
+
+        def spread_uv(c):
+            vb = spread(c, 1, "s")
+            u_bank[c] = spread(c, 0, "v")
+            v_rows[c] = work.tile([P, CH], BF16, name="v_rows", tag="v_rows")
+            nc.scalar.copy(out=v_rows[c][:], in_=vb[:])
+
+        def wave_tile(c, g):
+            if (c, g) not in wave:
+                wave[c, g] = work.tile([P, T, CH], F32, name="wave", tag="wave", bufs=CHUNKS * G)
+            return wave[c, g]
+
+        def jcols(rows, jt):
+            g, t = divmod(jt, T)
+            return rows[:, CH * g + t : CH * (g + 1) : T]
+
+        def sine(c, jt):
+            g, t = divmod(jt, T)
+            col = slice(jt, jt + 1)
+            if PE_FIRST <= c * JT + jt < PE_FIRST + PE_ARG:
+                b = bank("s", [P, CH], F32)
+                nc.tensor.matmul(out=b[:], lhsT=jcols(om_rows, jt), rhs=feat[c][:], start=True, stop=True)
+                nc.scalar.activation(out=wave_tile(c, g)[:, t, :], in_=b[:], func=ACT.Sin, bias=phi_f[:, col])
+            else:
+                arg = work.tile([P, CH], F32, name="arg", tag="arg", bufs=ARGB)
+                nc.vector.scalar_tensor_tensor(
+                    out=arg[:], in0=v_rows[c][:], scalar=ratio[:, col], in1=u_bank[c][:], op0=ALU.mult, op1=ALU.add
+                )
+                nc.scalar.activation(
+                    out=wave_tile(c, g)[:, t, :], in_=arg[:], func=ACT.Sin, bias=phi_f[:, col], scale=om0[:, col]
+                )
+
+        def feature_rows(c):
+            b = bank("s", [P, CH], BF16)
+            for n in range(TPC):
+                nc.tensor.transpose(b[:, P * n : P * (n + 1)], feat_t[:, TPC * c + n, :], ident_b[:])
+            feat[c] = const("feat%d" % c, [P, CH], BF16)
+            nc.scalar.copy(out=feat[c][:], in_=b[:])
+
+        tabs = {}
+
+        def window_tables():
+            gam_f = const("gam_f", [P, JT], F32)
+            nc.vector.tensor_copy(out=gam_f[:], in_=gam_j[:].rearrange("p g t -> p (g t)"))
+            mu2 = mu_j[:].rearrange("p a t -> p (a t)")
+            mu_sq = const("mu_sq", [P, 2 * JT], F32)
+            nc.vector.tensor_tensor(out=mu_sq[:], in0=mu2, in1=mu2, op=ALU.mult)
+            b1_f = const("b1_f", [P, JT], F32)
+            nc.vector.tensor_copy(out=b1_f[:], in_=b1_j[:].rearrange("p g t -> p (g t)"))
+            mu_n = const("mu_n", [P, JT], F32)
+            nc.vector.tensor_tensor(out=mu_n[:], in0=mu_sq[:, 0:JT], in1=mu_sq[:, JT : 2 * JT], op=ALU.add)
+            win_b = const("win_b", [P, JT], F32)
+            nc.vector.scalar_tensor_tensor(out=win_b[:], in0=mu_n[:], scalar=-0.5, in1=gam_f[:], op0=ALU.mult, op1=ALU.mult)
+            tabs["gam"], tabs["b1"], tabs["win_b"] = gam_f, b1_f, win_b
+
+        w1 = const("w1", [P, G * JT, 2 * P], U8)
+        s1 = const("s1", [P, G * JT, P], U8)
+
+        def sort_w1():
+            eng = nc.vector if W1_ENG == "V" else nc.gpsimd
+            eng.tensor_copy(
+                out=w1[:].rearrange("p (a t) (m b) -> p a t m b", t=T, b=2),
+                in_=w1_raw[:].rearrange("p g (h m t b) -> p (g h) t m b", h=G, t=T, b=2),
+            )
+            eng.tensor_copy(
+                out=s1[:].rearrange("p (a t) m -> p a t m", t=T),
+                in_=s1_raw[:].rearrange("p g (h m t) -> p (g h) t m", h=G, t=T),
+            )
+
+        scaled, z_in, z_q = {}, {}, {}
+
+        def scale(tile, level, eng):
+            s = work.tile([P, G, T, P], F32, name="scaled%d" % level, tag="scaled%d" % level, bufs=TPC)
+            k, r = divmod(tile, 2)
+            c, n = divmod(tile, TPC)
+            src = mips[k, level][:, r, :].rearrange("p (g m t) -> p g t m", g=G, t=T)
+            f = one_minus[k][:, r : r + 1] if level == 0 else frac_f[:, tile : tile + 1]
+            if eng == "S":
+                nc.scalar.activation(out=s[:], in_=src, func=ACT.Copy, scale=f)
+            elif eng == "V":
+                nc.vector.tensor_scalar(out=s[:], in0=src, scalar1=f, scalar2=None, op0=ALU.mult)
+            else:
+                nc.gpsimd.tensor_scalar(out=s[:], in0=src, scalar1=f, scalar2=0.0, op0=ALU.mult, op1=ALU.add)
+            scaled[c, n, level] = s
+
+        z_bank = {}
+
+        def turn(c, n, g):
+            b = bank("s", [P, T, P], F32)
+            for t in range(T):
+                for level in range(2):
+                    nc.tensor.matmul(
+                        out=b[:, t, :], lhsT=scaled[c, n, level][:, g, t, :], rhs=ident[:],
+                        is_transpose=True, start=(level == 0), stop=(level == 1),
+                    )
+            z_bank[c, n, g] = b
+
+        def empty_z(c, n, g):
+            if (c, g) not in z_in:
+                z_in[c, g] = work.tile([P, CH, T], BF16, name="z_in", tag="z_in", align_bytes=64)
+            dst = z_in[c, g][:, P * n : P * (n + 1), :]
+            src = z_bank[c, n, g][:].rearrange("p t i -> p i t")
+            if c == 0 and EV_HEAD[2 * n + g] == "V":
+                nc.vector.tensor_copy(out=dst, in_=src)
+            else:
+                nc.scalar.copy(out=dst, in_=src)
+
+        def quantise(src, tag, bufs):
+            codes = work.tile([P, CH], U32, name=tag, tag=tag, bufs=bufs, align_bytes=64)
+            scales = work.tile([P, CH], U8, name=tag + "_s", tag=tag + "_s", bufs=bufs, align_bytes=64)
+            nc.vector.quantize_mx(out=codes[:].bitcast(FP8X4), scales=scales[:], in_=src[:].rearrange("p i t -> p (i t)"))
+            return codes, scales
+
+        def quant_z(c, g):
+            z_q[c, g] = quantise(z_in[c, g], "z_q", 4)
+
+        a_bank, window, h_in, h_q, y_bank, y_sb, sq_t, norm2 = {}, {}, {}, {}, {}, {}, {}, {}
+
+        def first_mm(c, jt):
+            b = bank("v", [P, CH], F32)
+            for g in range(G):
+                nc.tensor.matmul_mx(
+                    out=b[:], lhsT=w1[:, g * JT + jt, :].bitcast(FP4X4), lhsT_scale=s1[:, g * JT + jt, :],
+                    rhs=z_q[c, g][0][:].bitcast(FP8X4), rhs_scale=z_q[c, g][1][:], start=(g == 0), stop=(g == G - 1),
+                )
+            a_bank[c, jt] = b
+
+        def times_wave(c, jt):
+            g, t = divmod(jt, T)
+            w = wave[c, g][:, t, :]
+            nc.vector.scalar_tensor_tensor(
+                out=w, in0=a_bank[c, jt][:], scalar=tabs["b1"][:, jt : jt + 1], in1=w, op0=ALU.add, op1=ALU.mult
+            )
+
+        e_bank = {}
+
+        def exponent(c, jt):
+            b = bank("s", [P, CH], F32)
+            nc.tensor.matmul(out=b[:], lhsT=jcols(mu_rows, jt), rhs=feat[c][:], start=True, stop=True)
+            e_bank[c, jt] = b
+
+        def gauss(c, jt):
+            g, t = divmod(jt, T)
+            if (c, g) not in window:
+                window[c, g] = work.tile([P, T, CH], F32, name="window", tag="window", align_bytes=64)
+            col = slice(jt, jt + 1)
+            nc.scalar.activation(
+                out=window[c, g][:, t, :], in_=e_bank[c, jt][:], func=ACT.Exp,
+                bias=tabs["win_b"][:, col], scale=tabs["gam"][:, col],
+            )
+
+        def times_window(c, g):
+            h = work.tile([P, CH, T], BF16, name="h_in", tag="hin", align_bytes=64)
+            nc.vector.tensor_tensor(
+                out=h[:].rearrange("p (i e) t -> p i t e", e=2),
+                in0=wave[c, g][:].rearrange("p t (i e) -> p i t e", e=2),
+                in1=window[c, g][:].rearrange("p t (i e) -> p i t e", e=2),
+                op=ALU.mult,
+            )
+            h_in[c, g] = h
+
+        def quant_h(c, g):
+            h_q[c, g] = quantise(h_in[c, g], "h_q", 2)
+
+        def second_mm(c, n):
+            b = bank("v", [P, C], F32)
+            cols = slice(P * n, P * (n + 1))
+            for g in range(G):
+                nc.tensor.matmul_mx(
+                    out=b[:], lhsT=h_q[c, g][0][:, cols].bitcast(FP8X4), lhsT_scale=h_q[c, g][1][:, cols],
+                    rhs=w2[:, g, :].bitcast(FP8X4), rhs_scale=s2[:, g, :], start=(g == 0), stop=(g == G - 1),
+                )
+            y_bank[c, n] = b
+
+        def add_b2(c, n):
+            if c not in y_sb:
+                y_sb[c] = work.tile([P, TPC, C], F32, name="y_sb", tag="wave", bufs=CHUNKS * G)
+            nc.vector.tensor_tensor(out=y_sb[c][:, n, :], in0=y_bank[c, n][:], in1=b2_bc[:], op=ALU.add)
+
+        def maps(c, n):
+            v = y_sb[c][:, n, 2 * PL : C]
+            nc.scalar.activation(out=v, in_=v, func=ACT.Tanh)
+
+        def store_maps(c):
+            nc.sync.dma_start(out=out1_v[:, TPC * c : TPC * (c + 1), :], in_=y_sb[c][:, :, 2 * PL : C])
+
+        def square(c):
+            sq_t[c] = work.tile([P, TPC, 2 * PL], F32, name="sq", tag="sq", bufs=1)
+            v = y_sb[c][:, :, 0 : 2 * PL]
+            if c + 1 < CHUNKS:
+                nc.scalar.activation(out=sq_t[c][:], in_=v, func=ACT.Square)
+            else:
+                nc.vector.tensor_tensor(out=sq_t[c][:], in0=v, in1=v, op=ALU.mult)
+
+        def sum_squares(c):
+            norm2[c] = const("norm2_%d" % c, [P, TPC, PL], F32)
+            nc.vector.tensor_tensor(out=norm2[c][:], in0=sq_t[c][:, :, 0:PL], in1=sq_t[c][:, :, PL : 2 * PL], op=ALU.add)
+
+        def inv_norm(c):
+            nc.scalar.activation(out=norm2[c][:], in_=norm2[c][:], func=ACT.Abs_reciprocal_sqrt, bias=1.0)
+
+        def normals(c, eng):
+            v = y_sb[c][:, :, 0 : 2 * PL].rearrange("p n (h x) -> p n h x", h=2)
+            eng.tensor_tensor(
+                out=v, in0=v, in1=norm2[c][:].unsqueeze(2).to_broadcast([P, TPC, 2, PL]), op=ALU.mult
+            )
+            nc.sync.dma_start(out=out0_v[:, TPC * c : TPC * (c + 1), :], in_=y_sb[c][:, :, 0 : 2 * PL])
+
+        def gauss4(c, g):
+            for jt in range(T * g, T * (g + 1)):
+                exponent(c, jt)
+                gauss(c, jt)
+
+        def z_tile(c, n):
+            for g in range(G):
+                turn(c, n, g)
+                empty_z(c, n, g)
+
+        def z_pair(k):
+            c, half = divmod(k, 2)
+            order = [(n, g) for g in range(G) for n in (2 * half, 2 * half + 1)]
+            for n, g in order:
+                turn(c, n, g)
+            for n, g in order:
+                empty_z(c, n, g)
+
+        def scale_pair0(k):
+            make_one_minus(k)
+            scale(2 * k, 0, "G")
+            scale(2 * k + 1, 0, "G")
+
+        spread_uv(0)
+        for jt in range(JT):
+            sine(0, jt)
+            if jt == 1:
+                feature_rows(1)
+            if jt == 4:
+                spread_uv(1)
+        sort_w1()
+        window_tables()
+        make_fractions()
+        make_one_minus(1)
+        for tile in range(4):
+            scale(tile, 0, "G")
+            scale(tile, 1, "G")
+        for jt in range(JT):
+            sine(1, jt)
+            if jt == 2:
+                spread_uv(2)
+        for jt in range(JT):
+            sine(2, jt)
+            if jt == 2:
+                spread_uv(3)
+            if jt in (3, 7):
+                z_tile(0, jt // 4)
+        load_mips(4)
+        load_mips(5)
+        for jt in range(JT):
+            sine(3, jt)
+            if jt < 3:
+                feature_rows((0, 2, 3)[jt])
+            if jt == ZP1:
+                z_pair(1)
+        gauss4(0, 0)
+        quant_z(0, 0)
+        quant_z(0, 1)
+        scale_pair0(2)
+        for jt in range(T):
+            first_mm(0, jt)
+
+        last = CHUNKS - 1
+        for c in range(CHUNKS):
+            nxt = c < last
+            ka, kb = 2 * c + 2, 2 * c + 3
+            if nxt:
+                scale(2 * ka + 1, 1, "G" if c > 0 else "S")
+                scale(2 * ka, 1, "S")
+                scale(2 * kb, 1, "S")
+            for jt in range(T):
+                times_wave(c, jt)
+                if c > 0 and jt < 2:
+                    second_mm(c - 1, jt + 2)
+                if c == 0:
+                    first_mm(c, jt + T)
+                elif jt >= 2:
+                    first_mm(c, jt + 2)
+            if c > 0:
+                for n in range(2, TPC):
+                    add_b2(c - 1, n)
+                    maps(c - 1, n)
+                    first_mm(c, n + T)
+                store_maps(c - 1)
+                square(c - 1)
+            gauss4(c, 1)
+            times_window(c, 0)
+            if nxt:
+                scale(2 * kb + 1, 1, TB1)
+                scale_pair0(kb)
+            elif EARLY:
+                sum_squares(c - 1)
+                for cc in range(last):
+                    inv_norm(cc)
+            for jt in range(T, JT):
+                times_wave(c, jt)
+            if nxt:
+                z_pair(ka)
+                z_pair(kb)
+                if c == 0:
+                    load_mips(6)
+                    load_mips(7)
+            quant_h(c, 0)
+            times_window(c, 1)
+            if nxt:
+                gauss4(c + 1, 0)
+            if 0 < c < last:
+                sum_squares(c - 1)
+            if not nxt:
+                normals(0, nc.vector)
+            quant_h(c, 1)
+            if nxt:
+                quant_z(c + 1, 0)
+                quant_z(c + 1, 1)
+            else:
+                normals(1, nc.vector)
+                normals(2, nc.vector)
+            if c + 2 < CHUNKS:
+                scale_pair0(ka + 2)
+            second_mm(c, 0)
+            second_mm(c, 1)
+            if nxt:
+                first_mm(c + 1, 0)
+                first_mm(c + 1, 1)
+            else:
+                second_mm(c, 2)
+                second_mm(c, 3)
+            for n in range(2):
+                add_b2(c, n)
+                maps(c, n)
+                if nxt:
+                    first_mm(c + 1, n + 2)
+        for n in range(2, TPC):
+            add_b2(last, n)
+            maps(last, n)
+        store_maps(last)
+        square(last)
+        sum_squares(last)
+        inv_norm(last)
+        normals(last, nc.vector)

@@ -25,8 +25,15 @@ G = 2
 T = 4
 JT = 8
 PE_ARG = 6
-EV_HEAD = "VVVVVVVV"
-PE_FIRST = 8
+EV = "VVVVVVVV" + "S" * 24
+SCB = 6
+LATE = 0
+FR = (5, 19, 21, 23)
+P3E = "GGGS"
+IT0_FULL = False
+Z0 = (11, 14, 17, 26)
+STRIDE_S = 1
+PE_FIRST = 18
 ARGB = 5
 ZP1 = 7
 TB1 = "S"
@@ -129,7 +136,6 @@ def tile_gabor_texture_decoder_f7_kernel(
         om_inv = const("om_inv", [P, JT], F32)
         ratio = const("ratio", [P, JT], F32)
         phi_f = const("phi_f", [P, JT], F32)
-        frac_f = const("frac_f", [P, TILES], F32)
         nc.vector.tensor_copy(out=uv_f[:], in_=uv_sb[:])
         nc.vector.tensor_tensor(out=uv_sq[:], in0=uv3, in1=uv3, op=ALU.mult)
         nc.vector.tensor_tensor(out=om_sq[:], in0=om_f[:, 0:JT], in1=om_f[:, 0:JT], op=ALU.mult)
@@ -142,18 +148,17 @@ def tile_gabor_texture_decoder_f7_kernel(
         nc.vector.tensor_copy(out=phi_f[:], in_=phi_j[:].rearrange("p g t -> p (g t)"))
         nc.vector.tensor_tensor(out=ratio[:], in0=om_f[:, JT : 2 * JT], in1=om_inv[:], op=ALU.mult)
 
-        one_minus = {}
+        factor = {}
 
-        def make_one_minus(c):
-            o = const("one_minus%d" % c, [P, 2], F32)
-            nc.vector.tensor_scalar(
-                out=o[:], in0=frac_f[:, 2 * c : 2 * (c + 1)], scalar1=-1.0, scalar2=1.0, op0=ALU.mult, op1=ALU.add
-            )
-            one_minus[c] = o
-
-        def make_fractions():
-            nc.vector.tensor_copy(out=frac_f[:], in_=frac_sb[:])
-            make_one_minus(0)
+        def make_factor(k, level, count=1):
+            o = const("factor%d_%d" % (k, level), [P, 2 * count], F32)
+            src = frac_sb[:, 2 * k : 2 * (k + count)]
+            if level == 0:
+                nc.vector.tensor_scalar(out=o[:], in0=src, scalar1=-1.0, scalar2=1.0, op0=ALU.mult, op1=ALU.add)
+            else:
+                nc.vector.tensor_copy(out=o[:], in_=src)
+            for r in range(2 * count):
+                factor[2 * k + r, level] = o[:, r : r + 1]
 
         u_bank, v_rows, wave, feat = {}, {}, {}, {}
 
@@ -235,11 +240,11 @@ def tile_gabor_texture_decoder_f7_kernel(
         scaled, z_in, z_q = {}, {}, {}
 
         def scale(tile, level, eng):
-            s = work.tile([P, G, T, P], F32, name="scaled%d" % level, tag="scaled%d" % level, bufs=TPC)
+            s = work.tile([P, G, T, P], F32, name="scaled%d" % level, tag="scaled%d" % level, bufs=SCB)
             k, r = divmod(tile, 2)
             c, n = divmod(tile, TPC)
             src = mips[k, level][:, r, :].rearrange("p (g m t) -> p g t m", g=G, t=T)
-            f = one_minus[k][:, r : r + 1] if level == 0 else frac_f[:, tile : tile + 1]
+            f = factor[tile, level]
             if eng == "S":
                 nc.scalar.activation(out=s[:], in_=src, func=ACT.Copy, scale=f)
             elif eng == "V":
@@ -265,7 +270,7 @@ def tile_gabor_texture_decoder_f7_kernel(
                 z_in[c, g] = work.tile([P, CH, T], BF16, name="z_in", tag="z_in", align_bytes=64)
             dst = z_in[c, g][:, P * n : P * (n + 1), :]
             src = z_bank[c, n, g][:].rearrange("p t i -> p i t")
-            if c == 0 and EV_HEAD[2 * n + g] == "V":
+            if EV[8 * c + 2 * n + g] == "V":
                 nc.vector.tensor_copy(out=dst, in_=src)
             else:
                 nc.scalar.copy(out=dst, in_=src)
@@ -346,8 +351,8 @@ def tile_gabor_texture_decoder_f7_kernel(
             v = y_sb[c][:, n, 2 * PL : C]
             nc.scalar.activation(out=v, in_=v, func=ACT.Tanh)
 
-        def store_maps(c):
-            nc.sync.dma_start(out=out1_v[:, TPC * c : TPC * (c + 1), :], in_=y_sb[c][:, :, 2 * PL : C])
+        def store_maps(c, n0=0, n1=TPC):
+            nc.sync.dma_start(out=out1_v[:, TPC * c + n0 : TPC * c + n1, :], in_=y_sb[c][:, n0:n1, 2 * PL : C])
 
         def square(c):
             sq_t[c] = work.tile([P, TPC, 2 * PL], F32, name="sq", tag="sq", bufs=1)
@@ -389,58 +394,58 @@ def tile_gabor_texture_decoder_f7_kernel(
             for n, g in order:
                 empty_z(c, n, g)
 
-        def scale_pair0(k):
-            make_one_minus(k)
-            scale(2 * k, 0, "G")
-            scale(2 * k + 1, 0, "G")
+        def scale_group(k, level, engines):
+            if (2 * k, level) not in factor:
+                make_factor(k, level)
+            for r in range(2):
+                scale(2 * k + r, level, engines[r])
 
         spread_uv(0)
-        for jt in range(JT):
-            sine(0, jt)
-            if jt == 1:
-                feature_rows(1)
-            if jt == 4:
-                spread_uv(1)
-        sort_w1()
-        window_tables()
-        make_fractions()
-        make_one_minus(1)
-        for tile in range(4):
-            scale(tile, 0, "G")
-            scale(tile, 1, "G")
-        for jt in range(JT):
-            sine(1, jt)
-            if jt == 2:
-                spread_uv(2)
-        for jt in range(JT):
-            sine(2, jt)
-            if jt == 2:
-                spread_uv(3)
-            if jt in (3, 7):
-                z_tile(0, jt // 4)
-        load_mips(4)
-        load_mips(5)
-        for jt in range(JT):
-            sine(3, jt)
-            if jt < 3:
-                feature_rows((0, 2, 3)[jt])
-            if jt == ZP1:
-                z_pair(1)
+        for step in range(CHUNKS * JT):
+            c, jt = divmod(step, JT)
+            if step == PE_FIRST:
+                sort_w1()
+                window_tables()
+                make_factor(2, 0)
+                for tile in range(TPC, TPC + 2):
+                    scale(tile, 0, "G")
+                    scale(tile, 1, "G")
+            sine(c, jt)
+            if jt == 1 and c + 1 < CHUNKS:
+                spread_uv(c + 1)
+            if step == 2:
+                make_factor(0, 0, 2)
+                make_factor(0, 1, 7)
+                for tile in range(TPC):
+                    scale(tile, 0, "G")
+                    scale(tile, 1, "G")
+            if step in Z0:
+                z_tile(0, Z0.index(step))
+            if step == Z0[1]:
+                load_mips(4)
+            if step == Z0[3]:
+                load_mips(5)
+            if step in FR:
+                feature_rows((2, 0, 1, 3)[FR.index(step)])
         gauss4(0, 0)
         quant_z(0, 0)
         quant_z(0, 1)
-        scale_pair0(2)
+        make_factor(3, 0)
+        for level in range(2):
+            for r in range(2):
+                scale(TPC + 2 + r, level, P3E[2 * level + r])
         for jt in range(T):
             first_mm(0, jt)
 
         last = CHUNKS - 1
+        W1 = ([], [(5, 0, "GG"), (5, 1, "GS")], [(7, 0, "GG"), (6, 1, "GS")], [])
+        W2 = ([(4, 0, "GG"), (4, 1, "SS")], [(6, 0, "GG")], [(7, 1, "GS")], [])
         for c in range(CHUNKS):
             nxt = c < last
             ka, kb = 2 * c + 2, 2 * c + 3
-            if nxt:
-                scale(2 * ka + 1, 1, "G" if c > 0 else "S")
-                scale(2 * ka, 1, "S")
-                scale(2 * kb, 1, "S")
+            if c == 0:
+                for k, level, engines in W1[c]:
+                    scale_group(k, level, engines)
             for jt in range(T):
                 times_wave(c, jt)
                 if c > 0 and jt < 2:
@@ -450,23 +455,30 @@ def tile_gabor_texture_decoder_f7_kernel(
                 elif jt >= 2:
                     first_mm(c, jt + 2)
             if c > 0:
-                for n in range(2, TPC):
+                for n in range(2, TPC - LATE):
                     add_b2(c - 1, n)
                     maps(c - 1, n)
                     first_mm(c, n + T)
-                store_maps(c - 1)
-                square(c - 1)
+                if not LATE:
+                    store_maps(c - 1)
+                    square(c - 1)
             gauss4(c, 1)
             times_window(c, 0)
-            if nxt:
-                scale(2 * kb + 1, 1, TB1)
-                scale_pair0(kb)
-            elif EARLY:
-                sum_squares(c - 1)
-                for cc in range(last):
-                    inv_norm(cc)
+            for k, level, engines in W2[c]:
+                if engines[0] == "G":
+                    scale_group(k, level, engines)
+            if c > 0 and LATE:
+                add_b2(c - 1, TPC - 1)
+                maps(c - 1, TPC - 1)
+                first_mm(c, JT - 1)
+                store_maps(c - 1)
+                square(c - 1)
             for jt in range(T, JT):
                 times_wave(c, jt)
+                if not nxt and jt == T + 1:
+                    sum_squares(c - 1)
+                    for cc in range(last):
+                        inv_norm(cc)
             if nxt:
                 z_pair(ka)
                 z_pair(kb)
@@ -477,6 +489,9 @@ def tile_gabor_texture_decoder_f7_kernel(
             times_window(c, 1)
             if nxt:
                 gauss4(c + 1, 0)
+            for k, level, engines in W2[c]:
+                if engines[0] == "S":
+                    scale_group(k, level, engines)
             if 0 < c < last:
                 sum_squares(c - 1)
             if not nxt:
@@ -487,14 +502,17 @@ def tile_gabor_texture_decoder_f7_kernel(
                 quant_z(c + 1, 1)
             else:
                 normals(1, nc.vector)
-                normals(2, nc.vector)
-            if c + 2 < CHUNKS:
-                scale_pair0(ka + 2)
             second_mm(c, 0)
             second_mm(c, 1)
             if nxt:
                 first_mm(c + 1, 0)
                 first_mm(c + 1, 1)
+                for k, level, engines in W1[c + 1]:
+                    if level == 0:
+                        make_factor(k, level)
+                    for r in range(2):
+                        if engines[r] == "G":
+                            scale(2 * k + r, level, "G")
             else:
                 second_mm(c, 2)
                 second_mm(c, 3)
@@ -503,11 +521,19 @@ def tile_gabor_texture_decoder_f7_kernel(
                 maps(c, n)
                 if nxt:
                     first_mm(c + 1, n + 2)
+            if nxt:
+                for k, level, engines in W1[c + 1]:
+                    for r in range(2):
+                        if engines[r] == "S":
+                            scale(2 * k + r, level, "S")
+            else:
+                store_maps(last, 0, 2)
         for n in range(2, TPC):
             add_b2(last, n)
             maps(last, n)
-        store_maps(last)
+            store_maps(last, n, n + 1)
         square(last)
+        normals(last - 1, nc.vector)
         sum_squares(last)
         inv_norm(last)
         normals(last, nc.vector)

@@ -24,16 +24,24 @@ CH = 512
 G = 2
 T = 4
 JT = 8
+PAD = 16
 PE_ARG = 6
-EV = "VVVVVVVV" + "S" * 24
+EV = "SVVVSVVV" + "S" * 24
 SCB = 6
+MAPS_FIRST = False
+SUM_EARLY = False
+NB = 4
+EARLY4 = 1
+NEXTRA = 2
 LATE = 0
-FR = (5, 19, 21, 23)
-P3E = "GGGS"
+FR = (12, 15, 19, 23)
+P3E = "GGGG"
+B2 = True
+TAILSPLIT = False
 IT0_FULL = False
-Z0 = (11, 14, 17, 26)
+Z0 = (11, 14, 18, 22)
 STRIDE_S = 1
-PE_FIRST = 18
+PE_FIRST = 26
 ARGB = 5
 ZP1 = 7
 TB1 = "S"
@@ -66,32 +74,23 @@ def tile_gabor_texture_decoder_f7_kernel(
         mu_rows = const("mu_rows", [P, N], BF16)
         feat_t = work.tile([P, TILES, P], BF16, name="feat_t", tag="hin", align_bytes=64)
         s2 = const("s2", [P, G, C], U8)
+        nc.vector.memset(feat_t[:].bitcast(I32), 0)
         nc.vector.memset(om_rows[:].bitcast(I32), 0)
         nc.vector.memset(s1_raw[:].bitcast(I32), 0)
-        nc.vector.memset(feat_t[:].bitcast(I32), 0)
         nc.vector.memset(mu_rows[:].bitcast(I32), 0)
-        nc.vector.memset(mu_rows[0:6, :], -0.5)
         nc.vector.memset(s2[:].bitcast(I32), 0)
+        nc.vector.memset(mu_rows[0:6, :], -0.5)
         ident = const("ident", [P, P], F32)
         make_identity(nc, ident[:])
 
         uv_sb = const("uv_sb", [P, TILES * 2], BF16)
         nc.sync.dma_start(out=uv_sb[:], in_=uv.rearrange("(p n) d -> p (n d)", n=TILES))
-        om_j = const("om_j", [P, 2 * G, T], BF16)
-        nc.scalar.dma_start(out=om_j[:], in_=omega.rearrange("d (g p t) -> p (d g) t", p=P, t=T))
-        phi_j = const("phi_j", [P, G, T], BF16)
-        nc.scalar.dma_start(out=phi_j[:], in_=phi.rearrange("(g p t) -> p g t", p=P, t=T))
-        nc.sync.dma_start(out=om_rows[0:2, :], in_=omega)
+        om_j = const("om_j", [P, 2 * G, PAD], BF16)[:, :, 0:T]
+        nc.sync.dma_start(out=om_j, in_=omega.rearrange("d (g p t) -> p (d g) t", p=P, t=T))
+        phi_j = const("phi_j", [P, G, PAD], BF16)[:, :, 0:T]
+        nc.sync.dma_start(out=phi_j, in_=phi.rearrange("(g p t) -> p g t", p=P, t=T))
         frac_sb = const("frac_sb", [P, TILES], BF16)
         nc.sync.dma_start(out=frac_sb[:], in_=frac.rearrange("(p n) -> p n", n=TILES))
-        w1_raw = work.tile([P, G, 2 * N], U8, name="w1_raw", tag="window", align_bytes=64)
-        nc.sync.dma_start(out=w1_raw[:].bitcast(I32), in_=w1_words.rearrange("g p b -> p g b").bitcast(I32))
-        for q in range(4):
-            nc.sync.dma_start(
-                out=s1_raw[32 * q : 32 * q + 4, :, :].bitcast(I32),
-                in_=w1_scales[:, 4 * q : 4 * q + 4, :].rearrange("g r n -> r g n").bitcast(I32),
-            )
-
         mips = {}
 
         def load_mips(k):
@@ -101,15 +100,23 @@ def tile_gabor_texture_decoder_f7_kernel(
                 mips[k, level] = m
 
         load_mips(0)
-        mu_j = const("mu_j", [P, 2 * G, T], BF16)
-        nc.sync.dma_start(out=mu_j[:], in_=mu.rearrange("d (g p t) -> p (d g) t", p=P, t=T))
-        gam_j = const("gam_j", [P, G, T], BF16)
-        nc.sync.dma_start(out=gam_j[:], in_=gamma.rearrange("(g p t) -> p g t", p=P, t=T))
-        b1_j = const("b1_j", [P, G, T], BF16)
-        nc.sync.dma_start(out=b1_j[:], in_=b1.rearrange("(g p t) -> p g t", p=P, t=T))
         load_mips(1)
-        nc.sync.dma_start(out=mu_rows[0:2, :], in_=mu)
         load_mips(2)
+        w1_raw = work.tile([P, G, 2 * N], U8, name="w1_raw", tag="window", align_bytes=64)
+        nc.sync.dma_start(out=w1_raw[:].bitcast(I32), in_=w1_words.rearrange("g p b -> p g b").bitcast(I32))
+        for q in range(4):
+            nc.sync.dma_start(
+                out=s1_raw[32 * q : 32 * q + 4, :, :].bitcast(I32),
+                in_=w1_scales[:, 4 * q : 4 * q + 4, :].rearrange("g r n -> r g n").bitcast(I32),
+            )
+        nc.sync.dma_start(out=om_rows[0:2, :], in_=omega)
+        mu_j = const("mu_j", [P, 2 * G, PAD], BF16)[:, :, 0:T]
+        nc.sync.dma_start(out=mu_j, in_=mu.rearrange("d (g p t) -> p (d g) t", p=P, t=T))
+        gam_j = const("gam_j", [P, G, PAD], BF16)[:, :, 0:T]
+        nc.sync.dma_start(out=gam_j, in_=gamma.rearrange("(g p t) -> p g t", p=P, t=T))
+        b1_j = const("b1_j", [P, G, PAD], BF16)[:, :, 0:T]
+        nc.sync.dma_start(out=b1_j, in_=b1.rearrange("(g p t) -> p g t", p=P, t=T))
+        nc.sync.dma_start(out=mu_rows[0:2, :], in_=mu)
         load_mips(3)
         w2 = const("w2", [P, G, C], U32)
         nc.sync.dma_start(out=w2[:].bitcast(I32), in_=w2_words.rearrange("g p n t -> p g (n t)").bitcast(I32))
@@ -123,13 +130,15 @@ def tile_gabor_texture_decoder_f7_kernel(
 
         warm = const("warm", [P, 1], F32)
         nc.scalar.activation(out=warm[:], in_=ident[:, 0:1], func=ACT.Sin)
-        ident_b = const("ident_b", [P, P], BF16)
-        nc.vector.tensor_copy(out=ident_b[:], in_=ident[:])
 
         uv_f = const("uv_f", [P, TILES * 2], F32)
         uv3 = uv_sb[:].rearrange("p (n d) -> p n d", d=2)
         uv_sq = const("uv_sq", [P, TILES, 2], F32)
-        om_f = om_j[:].rearrange("p a t -> p (a t)")
+        om_u, om_v = om_j[:, 0:G, :], om_j[:, G : 2 * G, :]
+
+        def by_g(table):
+            return table[:].rearrange("p (g t) -> p g t", t=T)
+
         om_sq = const("om_sq", [P, JT], F32)
         om_fix = const("om_fix", [P, JT], F32)
         om0 = const("om0", [P, JT], F32)
@@ -138,15 +147,18 @@ def tile_gabor_texture_decoder_f7_kernel(
         phi_f = const("phi_f", [P, JT], F32)
         nc.vector.tensor_copy(out=uv_f[:], in_=uv_sb[:])
         nc.vector.tensor_tensor(out=uv_sq[:], in0=uv3, in1=uv3, op=ALU.mult)
-        nc.vector.tensor_tensor(out=om_sq[:], in0=om_f[:, 0:JT], in1=om_f[:, 0:JT], op=ALU.mult)
+        nc.vector.tensor_tensor(out=by_g(om_sq), in0=om_u, in1=om_u, op=ALU.mult)
         nc.vector.tensor_copy(out=feat_t[:, :, 0:2], in_=uv3)
         nc.vector.tensor_scalar(out=om_fix[:], in0=om_sq[:], scalar1=2.0**-80, scalar2=2.0**-39, op0=ALU.is_lt, op1=ALU.mult)
         nc.vector.tensor_copy(out=feat_t[:, :, 2:4], in_=uv_sq[:])
-        nc.vector.tensor_tensor(out=om0[:], in0=om_f[:, 0:JT], in1=om_fix[:], op=ALU.add)
+        nc.vector.tensor_tensor(out=by_g(om0), in0=om_u, in1=by_g(om_fix), op=ALU.add)
         nc.vector.tensor_tensor(out=feat_t[:, :, 4:6], in0=uv_sq[:], in1=feat_t[:, :, 2:4], op=ALU.subtract)
         nc.vector.reciprocal(out=om_inv[:], in_=om0[:])
-        nc.vector.tensor_copy(out=phi_f[:], in_=phi_j[:].rearrange("p g t -> p (g t)"))
-        nc.vector.tensor_tensor(out=ratio[:], in0=om_f[:, JT : 2 * JT], in1=om_inv[:], op=ALU.mult)
+        nc.vector.tensor_copy(out=by_g(phi_f), in_=phi_j)
+        nc.vector.tensor_tensor(out=by_g(ratio), in0=om_v, in1=by_g(om_inv), op=ALU.mult)
+
+        ident_b = const("ident_b", [P, P], BF16)
+        nc.vector.tensor_copy(out=ident_b[:], in_=ident[:])
 
         factor = {}
 
@@ -211,12 +223,11 @@ def tile_gabor_texture_decoder_f7_kernel(
 
         def window_tables():
             gam_f = const("gam_f", [P, JT], F32)
-            nc.vector.tensor_copy(out=gam_f[:], in_=gam_j[:].rearrange("p g t -> p (g t)"))
-            mu2 = mu_j[:].rearrange("p a t -> p (a t)")
+            nc.vector.tensor_copy(out=by_g(gam_f), in_=gam_j)
             mu_sq = const("mu_sq", [P, 2 * JT], F32)
-            nc.vector.tensor_tensor(out=mu_sq[:], in0=mu2, in1=mu2, op=ALU.mult)
+            nc.vector.tensor_tensor(out=by_g(mu_sq), in0=mu_j, in1=mu_j, op=ALU.mult)
             b1_f = const("b1_f", [P, JT], F32)
-            nc.vector.tensor_copy(out=b1_f[:], in_=b1_j[:].rearrange("p g t -> p (g t)"))
+            nc.vector.tensor_copy(out=by_g(b1_f), in_=b1_j)
             mu_n = const("mu_n", [P, JT], F32)
             nc.vector.tensor_tensor(out=mu_n[:], in0=mu_sq[:, 0:JT], in1=mu_sq[:, JT : 2 * JT], op=ALU.add)
             win_b = const("win_b", [P, JT], F32)
@@ -286,8 +297,8 @@ def tile_gabor_texture_decoder_f7_kernel(
 
         a_bank, window, h_in, h_q, y_bank, y_sb, sq_t, norm2 = {}, {}, {}, {}, {}, {}, {}, {}
 
-        def first_mm(c, jt):
-            b = bank("v", [P, CH], F32)
+        def first_mm(c, jt, ring="v"):
+            b = bank(ring, [P, CH], F32)
             for g in range(G):
                 nc.tensor.matmul_mx(
                     out=b[:], lhsT=w1[:, g * JT + jt, :].bitcast(FP4X4), lhsT_scale=s1[:, g * JT + jt, :],
@@ -319,6 +330,17 @@ def tile_gabor_texture_decoder_f7_kernel(
                 bias=tabs["win_b"][:, col], scale=tabs["gam"][:, col],
             )
 
+        def add_b1(c, jt):
+            g, t = divmod(jt, T)
+            nc.scalar.activation(
+                out=wave[c, g][:, t, :], in_=a_bank[c, jt][:], func=ACT.Identity, bias=tabs["b1"][:, jt : jt + 1]
+            )
+
+        def gabor(c, g):
+            for t in range(0, NB, 2):
+                w = window[c, g][:, t : t + 2, :]
+                nc.gpsimd.tensor_tensor(out=w, in0=w, in1=wave[c, g][:, t : t + 2, :], op=ALU.mult)
+
         def times_window(c, g):
             h = work.tile([P, CH, T], BF16, name="h_in", tag="hin", align_bytes=64)
             nc.vector.tensor_tensor(
@@ -332,20 +354,24 @@ def tile_gabor_texture_decoder_f7_kernel(
         def quant_h(c, g):
             h_q[c, g] = quantise(h_in[c, g], "h_q", 2)
 
-        def second_mm(c, n):
-            b = bank("v", [P, C], F32)
+        def second_pass(c, n, g):
+            opens = (c, n) not in y_bank
+            if opens:
+                y_bank[c, n] = bank("v", [P, C], F32)
             cols = slice(P * n, P * (n + 1))
-            for g in range(G):
-                nc.tensor.matmul_mx(
-                    out=b[:], lhsT=h_q[c, g][0][:, cols].bitcast(FP8X4), lhsT_scale=h_q[c, g][1][:, cols],
-                    rhs=w2[:, g, :].bitcast(FP8X4), rhs_scale=s2[:, g, :], start=(g == 0), stop=(g == G - 1),
-                )
-            y_bank[c, n] = b
+            nc.tensor.matmul_mx(
+                out=y_bank[c, n][:], lhsT=h_q[c, g][0][:, cols].bitcast(FP8X4), lhsT_scale=h_q[c, g][1][:, cols],
+                rhs=w2[:, g, :].bitcast(FP8X4), rhs_scale=s2[:, g, :], start=opens, stop=not opens,
+            )
 
-        def add_b2(c, n):
+        def second_mm(c, n):
+            for g in range(G):
+                second_pass(c, n, g)
+
+        def add_b2(c, n, cols=slice(0, C)):
             if c not in y_sb:
                 y_sb[c] = work.tile([P, TPC, C], F32, name="y_sb", tag="wave", bufs=CHUNKS * G)
-            nc.vector.tensor_tensor(out=y_sb[c][:, n, :], in0=y_bank[c, n][:], in1=b2_bc[:], op=ALU.add)
+            nc.vector.tensor_tensor(out=y_sb[c][:, n, cols], in0=y_bank[c, n][:, cols], in1=b2_bc[:, cols], op=ALU.add)
 
         def maps(c, n):
             v = y_sb[c][:, n, 2 * PL : C]
@@ -386,12 +412,11 @@ def tile_gabor_texture_decoder_f7_kernel(
                 turn(c, n, g)
                 empty_z(c, n, g)
 
-        def z_pair(k):
+        def z_half(k, g):
             c, half = divmod(k, 2)
-            order = [(n, g) for g in range(G) for n in (2 * half, 2 * half + 1)]
-            for n, g in order:
+            for n in (2 * half, 2 * half + 1):
                 turn(c, n, g)
-            for n, g in order:
+            for n in (2 * half, 2 * half + 1):
                 empty_z(c, n, g)
 
         def scale_group(k, level, engines):
@@ -406,46 +431,44 @@ def tile_gabor_texture_decoder_f7_kernel(
             if step == PE_FIRST:
                 sort_w1()
                 window_tables()
-                make_factor(2, 0)
-                for tile in range(TPC, TPC + 2):
-                    scale(tile, 0, "G")
-                    scale(tile, 1, "G")
             sine(c, jt)
             if jt == 1 and c + 1 < CHUNKS:
                 spread_uv(c + 1)
-            if step == 2:
-                make_factor(0, 0, 2)
-                make_factor(0, 1, 7)
-                for tile in range(TPC):
+            if step == 0:
+                make_factor(0, 0, 4)
+                make_factor(0, 1, 8)
+                for tile in range(TPC + 2):
                     scale(tile, 0, "G")
                     scale(tile, 1, "G")
             if step in Z0:
                 z_tile(0, Z0.index(step))
             if step == Z0[1]:
+                for tile in range(TPC + 2, TPC + 2 + NEXTRA):
+                    scale(tile, 0, "G")
                 load_mips(4)
             if step == Z0[3]:
                 load_mips(5)
             if step in FR:
-                feature_rows((2, 0, 1, 3)[FR.index(step)])
+                feature_rows((3, 0, 1, 2)[FR.index(step)])
         gauss4(0, 0)
         quant_z(0, 0)
         quant_z(0, 1)
-        make_factor(3, 0)
-        for level in range(2):
+        make_factor(3, 1)
+        for level in (1, 0):
             for r in range(2):
-                scale(TPC + 2 + r, level, P3E[2 * level + r])
+                if level == 1 or r >= NEXTRA:
+                    scale(TPC + 2 + r, level, P3E[2 * level + r])
+        for r in range(EARLY4):
+            scale(8 + r, 1, "S")
         for jt in range(T):
             first_mm(0, jt)
 
         last = CHUNKS - 1
         W1 = ([], [(5, 0, "GG"), (5, 1, "GS")], [(7, 0, "GG"), (6, 1, "GS")], [])
-        W2 = ([(4, 0, "GG"), (4, 1, "SS")], [(6, 0, "GG")], [(7, 1, "GS")], [])
-        for c in range(CHUNKS):
-            nxt = c < last
+        W2 = ([(4, 0, "GG")], [(6, 0, "GG")], [], [])
+        for c in range(last):
             ka, kb = 2 * c + 2, 2 * c + 3
-            if c == 0:
-                for k, level, engines in W1[c]:
-                    scale_group(k, level, engines)
+            late = LATE if c > 0 else 0
             for jt in range(T):
                 times_wave(c, jt)
                 if c > 0 and jt < 2:
@@ -455,11 +478,11 @@ def tile_gabor_texture_decoder_f7_kernel(
                 elif jt >= 2:
                     first_mm(c, jt + 2)
             if c > 0:
-                for n in range(2, TPC - LATE):
+                for n in range(2, TPC - late):
                     add_b2(c - 1, n)
                     maps(c - 1, n)
                     first_mm(c, n + T)
-                if not LATE:
+                if not late:
                     store_maps(c - 1)
                     square(c - 1)
             gauss4(c, 1)
@@ -467,71 +490,155 @@ def tile_gabor_texture_decoder_f7_kernel(
             for k, level, engines in W2[c]:
                 if engines[0] == "G":
                     scale_group(k, level, engines)
-            if c > 0 and LATE:
+            if c == 2:
+                make_factor(7, 1)
+                scale(14, 1, "G")
+            if late:
                 add_b2(c - 1, TPC - 1)
-                maps(c - 1, TPC - 1)
+            z_half(ka, 0)
+            if late:
                 first_mm(c, JT - 1)
+                maps(c - 1, TPC - 1)
                 store_maps(c - 1)
                 square(c - 1)
             for jt in range(T, JT):
                 times_wave(c, jt)
-                if not nxt and jt == T + 1:
+            z_half(ka, 1)
+            z_half(kb, 0)
+            z_half(kb, 1)
+            if c == 0:
+                load_mips(6)
+                load_mips(7)
+            quant_h(c, 0)
+            times_window(c, 1)
+            held = B2 and c + 1 == last
+            for jt in range(T):
+                if not (held and jt == 1):
+                    exponent(c + 1, jt)
+                if not (held and jt >= 1):
+                    gauss(c + 1, jt)
+            if c == 0:
+                for r in range(EARLY4, 2):
+                    scale(8 + r, 1, "S")
+            if c > 0:
+                sum_squares(c - 1)
+            quant_h(c, 1)
+            quant_z(c + 1, 0)
+            quant_z(c + 1, 1)
+            first_g = T if (B2 and c + 1 == last) else 0
+            second_mm(c, 0)
+            if held:
+                exponent(last, 1)
+                for jt in range(1, T):
+                    gauss(last, jt)
+            second_mm(c, 1)
+            first_mm(c + 1, first_g)
+            first_mm(c + 1, first_g + 1)
+            for k, level, engines in W1[c + 1]:
+                if level == 0:
+                    make_factor(k, level)
+                for r in range(2):
+                    if engines[r] == "G":
+                        scale(2 * k + r, level, "G")
+            if B2 and c + 1 == last:
+                gabor(last, 0)
+                for jt in (T, T + 1):
+                    exponent(last, jt)
+                    gauss(last, jt)
+            for n in range(2):
+                add_b2(c, n)
+                first_mm(c + 1, first_g + n + 2)
+            if B2 and c + 1 == last:
+                for jt in (T + 2, T + 3):
+                    exponent(last, jt)
+                    gauss(last, jt)
+            for n in range(2):
+                maps(c, n)
+            for k, level, engines in W1[c + 1]:
+                for r in range(2):
+                    if engines[r] == "S":
+                        scale(2 * k + r, level, "S")
+            if c == 1:
+                scale(15, 1, "S")
+
+        c = last
+        if B2:
+            for jt in range(T, JT):
+                times_wave(c, jt)
+                if jt < T + 2:
+                    second_mm(c - 1, jt - 2)
+            for jt in range(NB, T):
+                first_mm(c, jt)
+            for n in range(2, TPC):
+                add_b2(c - 1, n)
+                if MAPS_FIRST:
+                    maps(c - 1, n)
+            for jt in range(NB):
+                first_mm(c, jt, "s")
+                add_b1(c, jt)
+            for jt in range(NB, T):
+                times_wave(c, jt)
+            for n in range(2, TPC):
+                if not MAPS_FIRST:
+                    maps(c - 1, n)
+            store_maps(c - 1)
+            square(c - 1)
+            times_window(c, 1)
+            if SUM_EARLY:
+                sum_squares(c - 1)
+            quant_h(c, 1)
+            for n in range(TPC):
+                second_pass(c, n, 1)
+            times_window(c, 0)
+            if not SUM_EARLY:
+                sum_squares(c - 1)
+            for cc in range(last):
+                inv_norm(cc)
+            if SUM_EARLY:
+                normals(0, nc.vector)
+            quant_h(c, 0)
+            for n in range(TPC):
+                second_pass(c, n, 0)
+            if not SUM_EARLY:
+                normals(0, nc.vector)
+            else:
+                normals(1, nc.vector)
+        else:
+            for jt in range(T):
+                times_wave(c, jt)
+                if jt < 2:
+                    second_mm(c - 1, jt + 2)
+                else:
+                    first_mm(c, jt + 2)
+            for n in range(2, TPC):
+                add_b2(c - 1, n)
+                maps(c - 1, n)
+                first_mm(c, n + T)
+            store_maps(c - 1)
+            square(c - 1)
+            gauss4(c, 1)
+            times_window(c, 0)
+            for jt in range(T, JT):
+                times_wave(c, jt)
+                if jt == T + 1:
                     sum_squares(c - 1)
                     for cc in range(last):
                         inv_norm(cc)
-            if nxt:
-                z_pair(ka)
-                z_pair(kb)
-                if c == 0:
-                    load_mips(6)
-                    load_mips(7)
             quant_h(c, 0)
             times_window(c, 1)
-            if nxt:
-                gauss4(c + 1, 0)
-            for k, level, engines in W2[c]:
-                if engines[0] == "S":
-                    scale_group(k, level, engines)
-            if 0 < c < last:
-                sum_squares(c - 1)
-            if not nxt:
-                normals(0, nc.vector)
+            normals(0, nc.vector)
             quant_h(c, 1)
-            if nxt:
-                quant_z(c + 1, 0)
-                quant_z(c + 1, 1)
-            else:
-                normals(1, nc.vector)
-            second_mm(c, 0)
-            second_mm(c, 1)
-            if nxt:
-                first_mm(c + 1, 0)
-                first_mm(c + 1, 1)
-                for k, level, engines in W1[c + 1]:
-                    if level == 0:
-                        make_factor(k, level)
-                    for r in range(2):
-                        if engines[r] == "G":
-                            scale(2 * k + r, level, "G")
-            else:
-                second_mm(c, 2)
-                second_mm(c, 3)
-            for n in range(2):
-                add_b2(c, n)
-                maps(c, n)
-                if nxt:
-                    first_mm(c + 1, n + 2)
-            if nxt:
-                for k, level, engines in W1[c + 1]:
-                    for r in range(2):
-                        if engines[r] == "S":
-                            scale(2 * k + r, level, "S")
-            else:
-                store_maps(last, 0, 2)
-        for n in range(2, TPC):
-            add_b2(last, n)
-            maps(last, n)
-            store_maps(last, n, n + 1)
+            normals(1, nc.vector)
+        for n in range(TPC):
+            add_b2(c, n, slice(2 * PL, C) if TAILSPLIT else slice(0, C))
+            maps(c, n)
+            if n > 0:
+                store_maps(c, 0 if n == 1 else n, n + 1)
+        if TAILSPLIT:
+            for n in range(TPC):
+                add_b2(c, n, slice(0, 2 * PL))
+        if not SUM_EARLY:
+            normals(1, nc.vector)
         square(last)
         normals(last - 1, nc.vector)
         sum_squares(last)

@@ -3,7 +3,7 @@ from contextlib import ExitStack
 import concourse.mybir as mybir
 from concourse.masks import make_identity
 
-M, L, N, C, PL = 2048, 1024, 1024, 512, 64
+M, L, N, C, PLANE = 2048, 1024, 1024, 512, 64
 FLOPS = 2 * M * L * N + 2 * M * N * C
 
 F32 = mybir.dt.float32
@@ -17,45 +17,32 @@ ALU = mybir.AluOpType
 ACT = mybir.ActivationFunctionType
 
 P = 128
-TILES = 16
-CHUNKS = 4
+SLOTS = 4
+GROUP = P * SLOTS
+GROUPS = L // GROUP
+JT = GROUPS * SLOTS
+TILES = M // P
 TPC = 4
-CH = 512
-G = 2
-T = 4
-JT = 8
-PAD = 16
-PE_ARG = 6
-EV = "SVVVSVVV" + "S" * 24
-SCB = 6
-MAPS_FIRST = False
-SUM_EARLY = False
-NB = 4
-EARLY4 = 1
-NEXTRA = 2
-LATE = 0
-FR = (12, 15, 19, 23)
-P3E = "GGGG"
-B2 = True
-TAILSPLIT = False
-IT0_FULL = False
-Z0 = (11, 14, 18, 22)
-STRIDE_S = 1
-PE_FIRST = 26
-ARGB = 5
-ZP1 = 7
-TB1 = "S"
-EARLY = True
-W1_ENG = "V"
+CHUNK = TPC * P
+CHUNKS = TILES // TPC
+LAST = CHUNKS - 1
+NORMAL = 2 * PLANE
+PARAM_ROW = 16
+FEATURES = 6
+
+PE_SINE_STEPS = 3
+BLEND_FIRST, BLEND_EVERY = 5, 2
+SCALAR_SHARE = 4
+SCALED_BUFS = 6
 
 
 def tile_gabor_texture_decoder_f7_kernel(
     tc, mip0, mip1, frac, uv, w1_words, w1_scales, b1, omega, phi, mu, gamma, w2_words, w2_scales, b2, out_0, out_1
 ):
     nc = tc.nc
-    mip_v = [m.rearrange("(p n) l -> p n l", n=TILES) for m in (mip0, mip1)]
-    out0_v = out_0.rearrange("(p n) c -> p n c", n=TILES)
-    out1_v = out_1.rearrange("(p n) c -> p n c", n=TILES)
+    mip_hbm = [m.rearrange("(p n) l -> p n l", n=TILES) for m in (mip0, mip1)]
+    normal_hbm = out_0.rearrange("(p n) c -> p n c", n=TILES)
+    maps_hbm = out_1.rearrange("(p n) c -> p n c", n=TILES)
 
     with ExitStack() as ctx:
         keep = ctx.enter_context(tc.tile_pool(name="keep", bufs=1))
@@ -66,293 +53,298 @@ def tile_gabor_texture_decoder_f7_kernel(
         def const(name, shape, dtype):
             return keep.tile(shape, dtype, name=name, align_bytes=64)
 
-        def bank(tag, shape, dtype):
-            return psum.tile(shape, dtype, name=tag, tag=tag)
+        def bank(ring, shape, dtype):
+            return psum.tile(shape, dtype, name=ring, tag=ring)
 
-        s1_raw = work.tile([P, G, N], U8, name="s1_raw", tag="window", align_bytes=64)
+        s1_raw = work.tile([P, GROUPS, N], U8, name="s1_raw", tag="window", align_bytes=64)
+        features_t = work.tile([P, TILES, P], BF16, name="features_t", tag="h_in", align_bytes=64)
         om_rows = const("om_rows", [P, N], BF16)
         mu_rows = const("mu_rows", [P, N], BF16)
-        feat_t = work.tile([P, TILES, P], BF16, name="feat_t", tag="hin", align_bytes=64)
-        s2 = const("s2", [P, G, C], U8)
-        nc.vector.memset(feat_t[:].bitcast(I32), 0)
+        s2 = const("s2", [P, GROUPS, C], U8)
+        nc.vector.memset(features_t[:].bitcast(I32), 0)
         nc.vector.memset(om_rows[:].bitcast(I32), 0)
         nc.vector.memset(s1_raw[:].bitcast(I32), 0)
         nc.vector.memset(mu_rows[:].bitcast(I32), 0)
         nc.vector.memset(s2[:].bitcast(I32), 0)
-        nc.vector.memset(mu_rows[0:6, :], -0.5)
+        nc.vector.memset(mu_rows[0:FEATURES, :], -0.5)
+        ident_b = const("ident_b", [P, P], BF16)
+        make_identity(nc, ident_b[:])
         ident = const("ident", [P, P], F32)
         make_identity(nc, ident[:])
 
-        uv_sb = const("uv_sb", [P, TILES * 2], BF16)
-        nc.sync.dma_start(out=uv_sb[:], in_=uv.rearrange("(p n) d -> p (n d)", n=TILES))
-        om_j = const("om_j", [P, 2 * G, PAD], BF16)[:, :, 0:T]
-        nc.sync.dma_start(out=om_j, in_=omega.rearrange("d (g p t) -> p (d g) t", p=P, t=T))
-        phi_j = const("phi_j", [P, G, PAD], BF16)[:, :, 0:T]
-        nc.sync.dma_start(out=phi_j, in_=phi.rearrange("(g p t) -> p g t", p=P, t=T))
-        frac_sb = const("frac_sb", [P, TILES], BF16)
-        nc.sync.dma_start(out=frac_sb[:], in_=frac.rearrange("(p n) -> p n", n=TILES))
+        def load_by_j(name, vec, rows):
+            dst = const(name, [P, rows * GROUPS, PARAM_ROW], BF16)[:, :, 0:SLOTS]
+            form = "d (g p t) -> p (d g) t" if rows > 1 else "(g p t) -> p g t"
+            nc.sync.dma_start(out=dst, in_=vec.rearrange(form, p=P, t=SLOTS))
+            return dst
+
+        def load_scales(plane, scales):
+            for q in range(4):
+                nc.sync.dma_start(
+                    out=plane[32 * q : 32 * q + 4, :, :].bitcast(I32),
+                    in_=scales[:, 4 * q : 4 * q + 4, :].rearrange("g r n -> r g n").bitcast(I32),
+                )
+
         mips = {}
 
-        def load_mips(k):
+        def load_mips(pair):
             for level in range(2):
                 m = work.tile([P, 2, L], BF16, name="mip%d" % level, tag="mip%d" % level, bufs=4)
-                nc.sync.dma_start(out=m[:], in_=mip_v[level][:, 2 * k : 2 * (k + 1), :])
-                mips[k, level] = m
+                nc.sync.dma_start(out=m[:], in_=mip_hbm[level][:, 2 * pair : 2 * (pair + 1), :])
+                mips[2 * pair, level], mips[2 * pair + 1, level] = m[:, 0, :], m[:, 1, :]
 
-        load_mips(0)
-        load_mips(1)
-        load_mips(2)
-        w1_raw = work.tile([P, G, 2 * N], U8, name="w1_raw", tag="window", align_bytes=64)
+        uv_sb = const("uv_sb", [P, TILES * 2], BF16)
+        nc.sync.dma_start(out=uv_sb[:], in_=uv.rearrange("(p n) d -> p (n d)", n=TILES))
+        om_j = load_by_j("om_j", omega, 2)
+        phi_j = load_by_j("phi_j", phi, 1)
+        frac_sb = const("frac_sb", [P, TILES], BF16)
+        nc.sync.dma_start(out=frac_sb[:], in_=frac.rearrange("(p n) -> p n", n=TILES))
+        for pair in range(3):
+            load_mips(pair)
+        w1_raw = work.tile([P, GROUPS, 2 * N], U8, name="w1_raw", tag="window", align_bytes=64)
         nc.sync.dma_start(out=w1_raw[:].bitcast(I32), in_=w1_words.rearrange("g p b -> p g b").bitcast(I32))
-        for q in range(4):
-            nc.sync.dma_start(
-                out=s1_raw[32 * q : 32 * q + 4, :, :].bitcast(I32),
-                in_=w1_scales[:, 4 * q : 4 * q + 4, :].rearrange("g r n -> r g n").bitcast(I32),
-            )
+        load_scales(s1_raw, w1_scales)
         nc.sync.dma_start(out=om_rows[0:2, :], in_=omega)
-        mu_j = const("mu_j", [P, 2 * G, PAD], BF16)[:, :, 0:T]
-        nc.sync.dma_start(out=mu_j, in_=mu.rearrange("d (g p t) -> p (d g) t", p=P, t=T))
-        gam_j = const("gam_j", [P, G, PAD], BF16)[:, :, 0:T]
-        nc.sync.dma_start(out=gam_j, in_=gamma.rearrange("(g p t) -> p g t", p=P, t=T))
-        b1_j = const("b1_j", [P, G, PAD], BF16)[:, :, 0:T]
-        nc.sync.dma_start(out=b1_j, in_=b1.rearrange("(g p t) -> p g t", p=P, t=T))
+        mu_j = load_by_j("mu_j", mu, 2)
+        gamma_j = load_by_j("gamma_j", gamma, 1)
+        b1_j = load_by_j("b1_j", b1, 1)
         nc.sync.dma_start(out=mu_rows[0:2, :], in_=mu)
         load_mips(3)
-        w2 = const("w2", [P, G, C], U32)
+        w2 = const("w2", [P, GROUPS, C], U32)
         nc.sync.dma_start(out=w2[:].bitcast(I32), in_=w2_words.rearrange("g p n t -> p g (n t)").bitcast(I32))
-        for q in range(4):
-            nc.sync.dma_start(
-                out=s2[32 * q : 32 * q + 4, :, :].bitcast(I32),
-                in_=w2_scales[:, 4 * q : 4 * q + 4, :].rearrange("g r n -> r g n").bitcast(I32),
-            )
+        load_scales(s2, w2_scales)
         b2_bc = const("b2_bc", [P, C], BF16)
         nc.sync.dma_start(out=b2_bc[:], in_=b2.partition_broadcast(P))
 
         warm = const("warm", [P, 1], F32)
-        nc.scalar.activation(out=warm[:], in_=ident[:, 0:1], func=ACT.Sin)
+        nc.scalar.activation(out=warm[:], in_=ident_b[:, 0:1], func=ACT.Sin)
 
-        uv_f = const("uv_f", [P, TILES * 2], F32)
+        def by_group(table):
+            return table[:].rearrange("p (g t) -> p g t", t=SLOTS)
+
         uv3 = uv_sb[:].rearrange("p (n d) -> p n d", d=2)
+        om_u, om_v = om_j[:, 0:GROUPS, :], om_j[:, GROUPS : 2 * GROUPS, :]
         uv_sq = const("uv_sq", [P, TILES, 2], F32)
-        om_u, om_v = om_j[:, 0:G, :], om_j[:, G : 2 * G, :]
-
-        def by_g(table):
-            return table[:].rearrange("p (g t) -> p g t", t=T)
-
         om_sq = const("om_sq", [P, JT], F32)
-        om_fix = const("om_fix", [P, JT], F32)
+        om_shift = const("om_shift", [P, JT], F32)
         om0 = const("om0", [P, JT], F32)
-        om_inv = const("om_inv", [P, JT], F32)
+        om0_inv = const("om0_inv", [P, JT], F32)
         ratio = const("ratio", [P, JT], F32)
         phi_f = const("phi_f", [P, JT], F32)
-        nc.vector.tensor_copy(out=uv_f[:], in_=uv_sb[:])
         nc.vector.tensor_tensor(out=uv_sq[:], in0=uv3, in1=uv3, op=ALU.mult)
-        nc.vector.tensor_tensor(out=by_g(om_sq), in0=om_u, in1=om_u, op=ALU.mult)
-        nc.vector.tensor_copy(out=feat_t[:, :, 0:2], in_=uv3)
-        nc.vector.tensor_scalar(out=om_fix[:], in0=om_sq[:], scalar1=2.0**-80, scalar2=2.0**-39, op0=ALU.is_lt, op1=ALU.mult)
-        nc.vector.tensor_copy(out=feat_t[:, :, 2:4], in_=uv_sq[:])
-        nc.vector.tensor_tensor(out=by_g(om0), in0=om_u, in1=by_g(om_fix), op=ALU.add)
-        nc.vector.tensor_tensor(out=feat_t[:, :, 4:6], in0=uv_sq[:], in1=feat_t[:, :, 2:4], op=ALU.subtract)
-        nc.vector.reciprocal(out=om_inv[:], in_=om0[:])
-        nc.vector.tensor_copy(out=by_g(phi_f), in_=phi_j)
-        nc.vector.tensor_tensor(out=by_g(ratio), in0=om_v, in1=by_g(om_inv), op=ALU.mult)
+        nc.vector.tensor_tensor(out=by_group(om_sq), in0=om_u, in1=om_u, op=ALU.mult)
+        nc.vector.tensor_copy(out=features_t[:, :, 0:2], in_=uv3)
+        nc.vector.tensor_scalar(
+            out=om_shift[:], in0=om_sq[:], scalar1=2.0**-80, scalar2=2.0**-39, op0=ALU.is_lt, op1=ALU.mult
+        )
+        nc.vector.tensor_copy(out=features_t[:, :, 2:4], in_=uv_sq[:])
+        nc.vector.tensor_tensor(out=by_group(om0), in0=om_u, in1=by_group(om_shift), op=ALU.add)
+        nc.vector.tensor_tensor(out=features_t[:, :, 4:6], in0=uv_sq[:], in1=features_t[:, :, 2:4], op=ALU.subtract)
+        nc.vector.reciprocal(out=om0_inv[:], in_=om0[:])
+        nc.vector.tensor_copy(out=by_group(phi_f), in_=phi_j)
+        nc.vector.tensor_tensor(out=by_group(ratio), in0=om_v, in1=by_group(om0_inv), op=ALU.mult)
 
-        ident_b = const("ident_b", [P, P], BF16)
-        nc.vector.tensor_copy(out=ident_b[:], in_=ident[:])
-
-        factor = {}
-
-        def make_factor(k, level, count=1):
-            o = const("factor%d_%d" % (k, level), [P, 2 * count], F32)
-            src = frac_sb[:, 2 * k : 2 * (k + count)]
-            if level == 0:
-                nc.vector.tensor_scalar(out=o[:], in0=src, scalar1=-1.0, scalar2=1.0, op0=ALU.mult, op1=ALU.add)
-            else:
-                nc.vector.tensor_copy(out=o[:], in_=src)
-            for r in range(2 * count):
-                factor[2 * k + r, level] = o[:, r : r + 1]
-
-        u_bank, v_rows, wave, feat = {}, {}, {}, {}
-
-        def spread(c, d, tag):
-            b = bank(tag, [P, CH], F32)
-            for n in range(TPC):
-                col = 2 * (TPC * c + n) + d
-                nc.tensor.transpose(b[:, P * n : P * (n + 1)], uv_f[:, col : col + 1].to_broadcast([P, P]), ident[:])
-            return b
-
-        def spread_uv(c):
-            vb = spread(c, 1, "s")
-            u_bank[c] = spread(c, 0, "v")
-            v_rows[c] = work.tile([P, CH], BF16, name="v_rows", tag="v_rows")
-            nc.scalar.copy(out=v_rows[c][:], in_=vb[:])
-
-        def wave_tile(c, g):
-            if (c, g) not in wave:
-                wave[c, g] = work.tile([P, T, CH], F32, name="wave", tag="wave", bufs=CHUNKS * G)
-            return wave[c, g]
-
-        def jcols(rows, jt):
-            g, t = divmod(jt, T)
-            return rows[:, CH * g + t : CH * (g + 1) : T]
-
-        def sine(c, jt):
-            g, t = divmod(jt, T)
-            col = slice(jt, jt + 1)
-            if PE_FIRST <= c * JT + jt < PE_FIRST + PE_ARG:
-                b = bank("s", [P, CH], F32)
-                nc.tensor.matmul(out=b[:], lhsT=jcols(om_rows, jt), rhs=feat[c][:], start=True, stop=True)
-                nc.scalar.activation(out=wave_tile(c, g)[:, t, :], in_=b[:], func=ACT.Sin, bias=phi_f[:, col])
-            else:
-                arg = work.tile([P, CH], F32, name="arg", tag="arg", bufs=ARGB)
-                nc.vector.scalar_tensor_tensor(
-                    out=arg[:], in0=v_rows[c][:], scalar=ratio[:, col], in1=u_bank[c][:], op0=ALU.mult, op1=ALU.add
-                )
-                nc.scalar.activation(
-                    out=wave_tile(c, g)[:, t, :], in_=arg[:], func=ACT.Sin, bias=phi_f[:, col], scale=om0[:, col]
-                )
-
-        def feature_rows(c):
-            b = bank("s", [P, CH], BF16)
-            for n in range(TPC):
-                nc.tensor.transpose(b[:, P * n : P * (n + 1)], feat_t[:, TPC * c + n, :], ident_b[:])
-            feat[c] = const("feat%d" % c, [P, CH], BF16)
-            nc.scalar.copy(out=feat[c][:], in_=b[:])
-
-        tabs = {}
+        gamma_f = const("gamma_f", [P, JT], F32)
+        b1_f = const("b1_f", [P, JT], F32)
+        window_bias = const("window_bias", [P, JT], F32)
 
         def window_tables():
-            gam_f = const("gam_f", [P, JT], F32)
-            nc.vector.tensor_copy(out=by_g(gam_f), in_=gam_j)
             mu_sq = const("mu_sq", [P, 2 * JT], F32)
-            nc.vector.tensor_tensor(out=by_g(mu_sq), in0=mu_j, in1=mu_j, op=ALU.mult)
-            b1_f = const("b1_f", [P, JT], F32)
-            nc.vector.tensor_copy(out=by_g(b1_f), in_=b1_j)
-            mu_n = const("mu_n", [P, JT], F32)
-            nc.vector.tensor_tensor(out=mu_n[:], in0=mu_sq[:, 0:JT], in1=mu_sq[:, JT : 2 * JT], op=ALU.add)
-            win_b = const("win_b", [P, JT], F32)
-            nc.vector.scalar_tensor_tensor(out=win_b[:], in0=mu_n[:], scalar=-0.5, in1=gam_f[:], op0=ALU.mult, op1=ALU.mult)
-            tabs["gam"], tabs["b1"], tabs["win_b"] = gam_f, b1_f, win_b
+            mu_norm = const("mu_norm", [P, JT], F32)
+            nc.vector.tensor_copy(out=by_group(gamma_f), in_=gamma_j)
+            nc.vector.tensor_tensor(out=by_group(mu_sq), in0=mu_j, in1=mu_j, op=ALU.mult)
+            nc.vector.tensor_copy(out=by_group(b1_f), in_=b1_j)
+            nc.vector.tensor_tensor(out=mu_norm[:], in0=mu_sq[:, 0:JT], in1=mu_sq[:, JT : 2 * JT], op=ALU.add)
+            nc.vector.scalar_tensor_tensor(
+                out=window_bias[:], in0=mu_norm[:], scalar=-0.5, in1=gamma_f[:], op0=ALU.mult, op1=ALU.mult
+            )
 
-        w1 = const("w1", [P, G * JT, 2 * P], U8)
-        s1 = const("s1", [P, G * JT, P], U8)
+        w1 = const("w1", [P, GROUPS * JT, 2 * P], U8)
+        s1 = const("s1", [P, GROUPS * JT, P], U8)
 
         def sort_w1():
-            eng = nc.vector if W1_ENG == "V" else nc.gpsimd
-            eng.tensor_copy(
-                out=w1[:].rearrange("p (a t) (m b) -> p a t m b", t=T, b=2),
-                in_=w1_raw[:].rearrange("p g (h m t b) -> p (g h) t m b", h=G, t=T, b=2),
+            nc.vector.tensor_copy(
+                out=w1[:].rearrange("p (a t) (m b) -> p a t m b", t=SLOTS, b=2),
+                in_=w1_raw[:].rearrange("p g (h m t b) -> p (g h) t m b", h=GROUPS, t=SLOTS, b=2),
             )
-            eng.tensor_copy(
-                out=s1[:].rearrange("p (a t) m -> p a t m", t=T),
-                in_=s1_raw[:].rearrange("p g (h m t) -> p (g h) t m", h=G, t=T),
+            nc.vector.tensor_copy(
+                out=s1[:].rearrange("p (a t) m -> p a t m", t=SLOTS),
+                in_=s1_raw[:].rearrange("p g (h m t) -> p (g h) t m", h=GROUPS, t=SLOTS),
             )
 
-        scaled, z_in, z_q = {}, {}, {}
+        hidden, hidden_half, u_bank, v_rows, features = {}, {}, {}, {}, {}
+        for half in range(2):
+            for g in range(GROUPS):
+                both = const("hidden%d_%d" % (half, g), [P, 2, SLOTS, CHUNK], F32)
+                hidden_half[half, g] = both
+                hidden[2 * half, g], hidden[2 * half + 1, g] = both[:, 0], both[:, 1]
 
-        def scale(tile, level, eng):
-            s = work.tile([P, G, T, P], F32, name="scaled%d" % level, tag="scaled%d" % level, bufs=SCB)
-            k, r = divmod(tile, 2)
-            c, n = divmod(tile, TPC)
-            src = mips[k, level][:, r, :].rearrange("p (g m t) -> p g t m", g=G, t=T)
-            f = factor[tile, level]
-            if eng == "S":
-                nc.scalar.activation(out=s[:], in_=src, func=ACT.Copy, scale=f)
-            elif eng == "V":
-                nc.vector.tensor_scalar(out=s[:], in0=src, scalar1=f, scalar2=None, op0=ALU.mult)
+        def spread(half, d, ring):
+            b = bank(ring, [P, 2 * CHUNK], BF16)
+            for n in range(2 * TPC):
+                col = 2 * (2 * TPC * half + n) + d
+                nc.tensor.transpose(b[:, P * n : P * (n + 1)], uv_sb[:, col : col + 1].to_broadcast([P, P]), ident_b[:])
+            return b
+
+        def spread_uv(half):
+            v_bank = spread(half, 1, "s")
+            u_bank[half] = spread(half, 0, "v")
+            v_rows[half] = work.tile([P, 2 * CHUNK], BF16, name="v_rows", tag="v_rows")
+            nc.scalar.copy(out=v_rows[half][:], in_=v_bank[:])
+
+        def feature_rows(half):
+            b = bank("s", [P, 2 * CHUNK], BF16)
+            for n in range(2 * TPC):
+                nc.tensor.transpose(b[:, P * n : P * (n + 1)], features_t[:, 2 * TPC * half + n, :], ident_b[:])
+            rows = const("features%d" % half, [P, 2 * CHUNK], BF16)
+            nc.scalar.copy(out=rows[:], in_=b[:])
+            features[2 * half], features[2 * half + 1] = rows[:, 0:CHUNK], rows[:, CHUNK : 2 * CHUNK]
+
+        def columns_of(rows, jt):
+            g, t = divmod(jt, SLOTS)
+            return rows[:, GROUP * g + t : GROUP * (g + 1) : SLOTS]
+
+        def sine_by_vector(half, jt):
+            g, t = divmod(jt, SLOTS)
+            col = slice(jt, jt + 1)
+            arg = work.tile([P, 2, CHUNK], F32, name="arg", tag="arg", bufs=3)
+            nc.vector.scalar_tensor_tensor(
+                out=arg[:].rearrange("p c i -> p (c i)"), in0=v_rows[half][:], scalar=ratio[:, col],
+                in1=u_bank[half][:], op0=ALU.mult, op1=ALU.add,
+            )
+            nc.scalar.activation(
+                out=hidden_half[half, g][:, :, t, :], in_=arg[:], func=ACT.Sin, bias=phi_f[:, col], scale=om0[:, col]
+            )
+
+        def sine_by_matmul(half, jt):
+            g, t = divmod(jt, SLOTS)
+            for c in (2 * half, 2 * half + 1):
+                b = bank("s", [P, CHUNK], F32)
+                nc.tensor.matmul(out=b[:], lhsT=columns_of(om_rows, jt), rhs=features[c], start=True, stop=True)
+                nc.scalar.activation(out=hidden[c, g][:, t, :], in_=b[:], func=ACT.Sin, bias=phi_f[:, jt : jt + 1])
+
+        frac_f = const("frac_f", [P, TILES], F32)
+        one_minus, scaled, z_bank, z_in, z_q = {}, {}, {}, {}, {}
+
+        def make_one_minus(first, count):
+            o = const("one_minus%d" % first, [P, count], F32)
+            nc.vector.tensor_scalar(
+                out=o[:], in0=frac_sb[:, first : first + count], scalar1=-1.0, scalar2=1.0, op0=ALU.mult, op1=ALU.add
+            )
+            for r in range(count):
+                one_minus[first + r] = o[:, r : r + 1]
+
+        def scale(tile, level, on_scalar=False):
+            s = work.tile([P, GROUPS, SLOTS, P], F32, name="scaled%d" % level, tag="scaled%d" % level, bufs=SCALED_BUFS)
+            src = mips[tile, level].rearrange("p (g m t) -> p g t m", g=GROUPS, t=SLOTS)
+            factor = one_minus[tile] if level == 0 else frac_f[:, tile : tile + 1]
+            if on_scalar:
+                nc.scalar.activation(out=s[:], in_=src, func=ACT.Copy, scale=factor)
             else:
-                nc.gpsimd.tensor_scalar(out=s[:], in0=src, scalar1=f, scalar2=0.0, op0=ALU.mult, op1=ALU.add)
-            scaled[c, n, level] = s
+                nc.gpsimd.tensor_scalar(out=s[:], in0=src, scalar1=factor, scalar2=0.0, op0=ALU.mult, op1=ALU.add)
+            scaled[tile, level] = s
 
-        z_bank = {}
-
-        def turn(c, n, g):
-            b = bank("s", [P, T, P], F32)
-            for t in range(T):
+        def blend(tile, g):
+            b = bank("s", [P, SLOTS, P], F32)
+            for t in range(SLOTS):
                 for level in range(2):
                     nc.tensor.matmul(
-                        out=b[:, t, :], lhsT=scaled[c, n, level][:, g, t, :], rhs=ident[:],
+                        out=b[:, t, :], lhsT=scaled[tile, level][:, g, t, :], rhs=ident[:],
                         is_transpose=True, start=(level == 0), stop=(level == 1),
                     )
-            z_bank[c, n, g] = b
+            z_bank[tile, g] = b
 
-        def empty_z(c, n, g):
+        def round_z(tile, g):
+            c, n = divmod(tile, TPC)
             if (c, g) not in z_in:
-                z_in[c, g] = work.tile([P, CH, T], BF16, name="z_in", tag="z_in", align_bytes=64)
+                z_in[c, g] = work.tile([P, CHUNK, SLOTS], BF16, name="z_in", tag="z_in", align_bytes=64)
             dst = z_in[c, g][:, P * n : P * (n + 1), :]
-            src = z_bank[c, n, g][:].rearrange("p t i -> p i t")
-            if EV[8 * c + 2 * n + g] == "V":
+            src = z_bank[tile, g][:].rearrange("p t i -> p i t")
+            if c == 0 and (GROUPS * n + g) % SCALAR_SHARE != 0:
                 nc.vector.tensor_copy(out=dst, in_=src)
             else:
                 nc.scalar.copy(out=dst, in_=src)
 
+        def blend_pair(first, g):
+            for tile in (first, first + 1):
+                blend(tile, g)
+            for tile in (first, first + 1):
+                round_z(tile, g)
+
         def quantise(src, tag, bufs):
-            codes = work.tile([P, CH], U32, name=tag, tag=tag, bufs=bufs, align_bytes=64)
-            scales = work.tile([P, CH], U8, name=tag + "_s", tag=tag + "_s", bufs=bufs, align_bytes=64)
+            codes = work.tile([P, CHUNK], U32, name=tag, tag=tag, bufs=bufs, align_bytes=64)
+            scales = work.tile([P, CHUNK], U8, name=tag + "_s", tag=tag + "_s", bufs=bufs, align_bytes=64)
             nc.vector.quantize_mx(out=codes[:].bitcast(FP8X4), scales=scales[:], in_=src[:].rearrange("p i t -> p (i t)"))
             return codes, scales
 
-        def quant_z(c, g):
-            z_q[c, g] = quantise(z_in[c, g], "z_q", 4)
+        def quantise_z(c):
+            for g in range(GROUPS):
+                z_q[c, g] = quantise(z_in[c, g], "z_q", 2 * GROUPS)
 
-        a_bank, window, h_in, h_q, y_bank, y_sb, sq_t, norm2 = {}, {}, {}, {}, {}, {}, {}, {}
+        a_bank, e_bank, window, h_in, h_q = {}, {}, {}, {}, {}
 
-        def first_mm(c, jt, ring="v"):
-            b = bank(ring, [P, CH], F32)
-            for g in range(G):
+        def first_matmul(c, jt, ring="v"):
+            b = bank(ring, [P, CHUNK], F32)
+            for g in range(GROUPS):
                 nc.tensor.matmul_mx(
                     out=b[:], lhsT=w1[:, g * JT + jt, :].bitcast(FP4X4), lhsT_scale=s1[:, g * JT + jt, :],
-                    rhs=z_q[c, g][0][:].bitcast(FP8X4), rhs_scale=z_q[c, g][1][:], start=(g == 0), stop=(g == G - 1),
+                    rhs=z_q[c, g][0][:].bitcast(FP8X4), rhs_scale=z_q[c, g][1][:],
+                    start=(g == 0), stop=(g == GROUPS - 1),
                 )
             a_bank[c, jt] = b
 
         def times_wave(c, jt):
-            g, t = divmod(jt, T)
-            w = wave[c, g][:, t, :]
+            g, t = divmod(jt, SLOTS)
+            w = hidden[c, g][:, t, :]
             nc.vector.scalar_tensor_tensor(
-                out=w, in0=a_bank[c, jt][:], scalar=tabs["b1"][:, jt : jt + 1], in1=w, op0=ALU.add, op1=ALU.mult
+                out=w, in0=a_bank[c, jt][:], scalar=b1_f[:, jt : jt + 1], in1=w, op0=ALU.add, op1=ALU.mult
             )
 
-        e_bank = {}
-
         def exponent(c, jt):
-            b = bank("s", [P, CH], F32)
-            nc.tensor.matmul(out=b[:], lhsT=jcols(mu_rows, jt), rhs=feat[c][:], start=True, stop=True)
+            b = bank("s", [P, CHUNK], F32)
+            nc.tensor.matmul(out=b[:], lhsT=columns_of(mu_rows, jt), rhs=features[c], start=True, stop=True)
             e_bank[c, jt] = b
 
         def gauss(c, jt):
-            g, t = divmod(jt, T)
+            g, t = divmod(jt, SLOTS)
             if (c, g) not in window:
-                window[c, g] = work.tile([P, T, CH], F32, name="window", tag="window", align_bytes=64)
+                window[c, g] = work.tile([P, SLOTS, CHUNK], F32, name="window", tag="window", align_bytes=64)
             col = slice(jt, jt + 1)
             nc.scalar.activation(
                 out=window[c, g][:, t, :], in_=e_bank[c, jt][:], func=ACT.Exp,
-                bias=tabs["win_b"][:, col], scale=tabs["gam"][:, col],
+                bias=window_bias[:, col], scale=gamma_f[:, col],
             )
+
+        def windows(c, jts):
+            for jt in jts:
+                exponent(c, jt)
+                gauss(c, jt)
+
+        def wave_into_window(c, g):
+            for t in range(0, SLOTS, 2):
+                w = window[c, g][:, t : t + 2, :]
+                nc.gpsimd.tensor_tensor(out=w, in0=w, in1=hidden[c, g][:, t : t + 2, :], op=ALU.mult)
 
         def add_b1(c, jt):
-            g, t = divmod(jt, T)
+            g, t = divmod(jt, SLOTS)
             nc.scalar.activation(
-                out=wave[c, g][:, t, :], in_=a_bank[c, jt][:], func=ACT.Identity, bias=tabs["b1"][:, jt : jt + 1]
+                out=hidden[c, g][:, t, :], in_=a_bank[c, jt][:], func=ACT.Identity, bias=b1_f[:, jt : jt + 1]
             )
 
-        def gabor(c, g):
-            for t in range(0, NB, 2):
-                w = window[c, g][:, t : t + 2, :]
-                nc.gpsimd.tensor_tensor(out=w, in0=w, in1=wave[c, g][:, t : t + 2, :], op=ALU.mult)
-
         def times_window(c, g):
-            h = work.tile([P, CH, T], BF16, name="h_in", tag="hin", align_bytes=64)
+            h = work.tile([P, CHUNK, SLOTS], BF16, name="h_in", tag="h_in", align_bytes=64)
             nc.vector.tensor_tensor(
                 out=h[:].rearrange("p (i e) t -> p i t e", e=2),
-                in0=wave[c, g][:].rearrange("p t (i e) -> p i t e", e=2),
+                in0=hidden[c, g].rearrange("p t (i e) -> p i t e", e=2),
                 in1=window[c, g][:].rearrange("p t (i e) -> p i t e", e=2),
                 op=ALU.mult,
             )
             h_in[c, g] = h
 
-        def quant_h(c, g):
-            h_q[c, g] = quantise(h_in[c, g], "h_q", 2)
+        def quantise_h(c, g):
+            h_q[c, g] = quantise(h_in[c, g], "h_q", GROUPS)
+
+        y_bank, squares, norm = {}, {}, {}
 
         def second_pass(c, n, g):
             opens = (c, n) not in y_bank
@@ -364,283 +356,201 @@ def tile_gabor_texture_decoder_f7_kernel(
                 rhs=w2[:, g, :].bitcast(FP8X4), rhs_scale=s2[:, g, :], start=opens, stop=not opens,
             )
 
-        def second_mm(c, n):
-            for g in range(G):
+        def second_matmul(c, n):
+            for g in range(GROUPS):
                 second_pass(c, n, g)
 
-        def add_b2(c, n, cols=slice(0, C)):
-            if c not in y_sb:
-                y_sb[c] = work.tile([P, TPC, C], F32, name="y_sb", tag="wave", bufs=CHUNKS * G)
-            nc.vector.tensor_tensor(out=y_sb[c][:, n, cols], in0=y_bank[c, n][:, cols], in1=b2_bc[:, cols], op=ALU.add)
+        def add_b2(c, n):
+            nc.vector.tensor_tensor(out=hidden[c, 0][:, n, :], in0=y_bank[c, n][:], in1=b2_bc[:], op=ALU.add)
 
         def maps(c, n):
-            v = y_sb[c][:, n, 2 * PL : C]
+            v = hidden[c, 0][:, n, NORMAL:C]
             nc.scalar.activation(out=v, in_=v, func=ACT.Tanh)
 
-        def store_maps(c, n0=0, n1=TPC):
-            nc.sync.dma_start(out=out1_v[:, TPC * c + n0 : TPC * c + n1, :], in_=y_sb[c][:, n0:n1, 2 * PL : C])
+        def store_maps(c, n0, n1):
+            nc.sync.dma_start(out=maps_hbm[:, TPC * c + n0 : TPC * c + n1, :], in_=hidden[c, 0][:, n0:n1, NORMAL:C])
 
         def square(c):
-            sq_t[c] = work.tile([P, TPC, 2 * PL], F32, name="sq", tag="sq", bufs=1)
-            v = y_sb[c][:, :, 0 : 2 * PL]
-            if c + 1 < CHUNKS:
-                nc.scalar.activation(out=sq_t[c][:], in_=v, func=ACT.Square)
+            squares[c] = work.tile([P, TPC, NORMAL], F32, name="squares", tag="squares", bufs=1)
+            v = hidden[c, 0][:, :, 0:NORMAL]
+            if c < LAST:
+                nc.scalar.activation(out=squares[c][:], in_=v, func=ACT.Square)
             else:
-                nc.vector.tensor_tensor(out=sq_t[c][:], in0=v, in1=v, op=ALU.mult)
+                nc.vector.tensor_tensor(out=squares[c][:], in0=v, in1=v, op=ALU.mult)
 
         def sum_squares(c):
-            norm2[c] = const("norm2_%d" % c, [P, TPC, PL], F32)
-            nc.vector.tensor_tensor(out=norm2[c][:], in0=sq_t[c][:, :, 0:PL], in1=sq_t[c][:, :, PL : 2 * PL], op=ALU.add)
-
-        def inv_norm(c):
-            nc.scalar.activation(out=norm2[c][:], in_=norm2[c][:], func=ACT.Abs_reciprocal_sqrt, bias=1.0)
-
-        def normals(c, eng):
-            v = y_sb[c][:, :, 0 : 2 * PL].rearrange("p n (h x) -> p n h x", h=2)
-            eng.tensor_tensor(
-                out=v, in0=v, in1=norm2[c][:].unsqueeze(2).to_broadcast([P, TPC, 2, PL]), op=ALU.mult
+            norm[c] = const("norm%d" % c, [P, TPC, PLANE], F32)
+            nc.vector.tensor_tensor(
+                out=norm[c][:], in0=squares[c][:, :, 0:PLANE], in1=squares[c][:, :, PLANE:NORMAL], op=ALU.add
             )
-            nc.sync.dma_start(out=out0_v[:, TPC * c : TPC * (c + 1), :], in_=y_sb[c][:, :, 0 : 2 * PL])
 
-        def gauss4(c, g):
-            for jt in range(T * g, T * (g + 1)):
-                exponent(c, jt)
-                gauss(c, jt)
+        def inverse_root(c):
+            nc.scalar.activation(out=norm[c][:], in_=norm[c][:], func=ACT.Abs_reciprocal_sqrt, bias=1.0)
 
-        def z_tile(c, n):
-            for g in range(G):
-                turn(c, n, g)
-                empty_z(c, n, g)
+        def normals(c):
+            v = hidden[c, 0][:, :, 0:NORMAL].rearrange("p n (h x) -> p n h x", h=2)
+            r = norm[c][:].unsqueeze(2).to_broadcast([P, TPC, 2, PLANE])
+            nc.vector.tensor_tensor(out=v, in0=v, in1=r, op=ALU.mult)
+            nc.sync.dma_start(out=normal_hbm[:, TPC * c : TPC * (c + 1), :], in_=hidden[c, 0][:, :, 0:NORMAL])
 
-        def z_half(k, g):
-            c, half = divmod(k, 2)
-            for n in (2 * half, 2 * half + 1):
-                turn(c, n, g)
-            for n in (2 * half, 2 * half + 1):
-                empty_z(c, n, g)
-
-        def scale_group(k, level, engines):
-            if (2 * k, level) not in factor:
-                make_factor(k, level)
-            for r in range(2):
-                scale(2 * k + r, level, engines[r])
-
+        make_one_minus(0, SCALED_BUFS)
+        nc.vector.tensor_copy(out=frac_f[:], in_=frac_sb[:])
         spread_uv(0)
-        for step in range(CHUNKS * JT):
-            c, jt = divmod(step, JT)
-            if step == PE_FIRST:
+        steps = 2 * JT
+        blend_steps = [BLEND_FIRST + BLEND_EVERY * n for n in range(TPC)]
+        for step in range(steps):
+            half, jt = divmod(step, JT)
+            if step == steps - PE_SINE_STEPS:
                 sort_w1()
-                window_tables()
-            sine(c, jt)
-            if jt == 1 and c + 1 < CHUNKS:
-                spread_uv(c + 1)
+            if step < steps - PE_SINE_STEPS:
+                sine_by_vector(half, jt)
+            else:
+                sine_by_matmul(half, jt)
             if step == 0:
-                make_factor(0, 0, 4)
-                make_factor(0, 1, 8)
-                for tile in range(TPC + 2):
-                    scale(tile, 0, "G")
-                    scale(tile, 1, "G")
-            if step in Z0:
-                z_tile(0, Z0.index(step))
-            if step == Z0[1]:
-                for tile in range(TPC + 2, TPC + 2 + NEXTRA):
-                    scale(tile, 0, "G")
-                load_mips(4)
-            if step == Z0[3]:
-                load_mips(5)
-            if step in FR:
-                feature_rows((3, 0, 1, 2)[FR.index(step)])
-        gauss4(0, 0)
-        quant_z(0, 0)
-        quant_z(0, 1)
-        make_factor(3, 1)
-        for level in (1, 0):
-            for r in range(2):
-                if level == 1 or r >= NEXTRA:
-                    scale(TPC + 2 + r, level, P3E[2 * level + r])
-        for r in range(EARLY4):
-            scale(8 + r, 1, "S")
-        for jt in range(T):
-            first_mm(0, jt)
+                for tile in range(SCALED_BUFS):
+                    scale(tile, 0)
+                    scale(tile, 1)
+            if step == 2:
+                spread_uv(1)
+            if step in blend_steps:
+                n = blend_steps.index(step)
+                for g in range(GROUPS):
+                    blend(n, g)
+                    round_z(n, g)
+                if n == 1:
+                    scale(SCALED_BUFS, 1)
+                    scale(SCALED_BUFS + 1, 1)
+                if n % 2 == 1:
+                    load_mips(4 + n // 2)
+            if step - 1 in blend_steps[0::2]:
+                feature_rows(1 - blend_steps.index(step - 1) // 2)
+        quantise_z(0)
+        window_tables()
+        windows(0, range(SLOTS))
+        make_one_minus(TPC + 2, 2)
+        scale(TPC + 2, 0)
+        scale(TPC + 3, 0)
+        scale(2 * TPC, 1, on_scalar=True)
+        for jt in range(SLOTS):
+            first_matmul(0, jt)
 
-        last = CHUNKS - 1
-        W1 = ([], [(5, 0, "GG"), (5, 1, "GS")], [(7, 0, "GG"), (6, 1, "GS")], [])
-        W2 = ([(4, 0, "GG")], [(6, 0, "GG")], [], [])
-        for c in range(last):
-            ka, kb = 2 * c + 2, 2 * c + 3
-            late = LATE if c > 0 else 0
-            for jt in range(T):
+        for c in range(LAST):
+            ahead = TPC * (c + 1)
+            for jt in range(SLOTS):
                 times_wave(c, jt)
-                if c > 0 and jt < 2:
-                    second_mm(c - 1, jt + 2)
                 if c == 0:
-                    first_mm(c, jt + T)
-                elif jt >= 2:
-                    first_mm(c, jt + 2)
+                    first_matmul(c, jt + SLOTS)
+                elif jt < 2:
+                    second_matmul(c - 1, jt + 2)
+                else:
+                    first_matmul(c, jt + 2)
             if c > 0:
-                for n in range(2, TPC - late):
+                for n in range(2, TPC):
                     add_b2(c - 1, n)
                     maps(c - 1, n)
-                    first_mm(c, n + T)
-                if not late:
-                    store_maps(c - 1)
-                    square(c - 1)
-            gauss4(c, 1)
-            times_window(c, 0)
-            for k, level, engines in W2[c]:
-                if engines[0] == "G":
-                    scale_group(k, level, engines)
-            if c == 2:
-                make_factor(7, 1)
-                scale(14, 1, "G")
-            if late:
-                add_b2(c - 1, TPC - 1)
-            z_half(ka, 0)
-            if late:
-                first_mm(c, JT - 1)
-                maps(c - 1, TPC - 1)
-                store_maps(c - 1)
+                    first_matmul(c, n + SLOTS)
+                store_maps(c - 1, 0, TPC)
                 square(c - 1)
-            for jt in range(T, JT):
+            windows(c, range(SLOTS, JT))
+            times_window(c, 0)
+            if c + 1 < LAST:
+                make_one_minus(ahead + TPC, 2)
+                scale(ahead + TPC, 0)
+                scale(ahead + TPC + 1, 0)
+            else:
+                make_one_minus(TILES - 1, 1)
+                scale(TILES - 1, 0)
+            blend_pair(ahead, 0)
+            for jt in range(SLOTS, JT):
                 times_wave(c, jt)
-            z_half(ka, 1)
-            z_half(kb, 0)
-            z_half(kb, 1)
+            blend_pair(ahead, 1)
+            blend_pair(ahead + 2, 0)
+            blend_pair(ahead + 2, 1)
             if c == 0:
                 load_mips(6)
                 load_mips(7)
-            quant_h(c, 0)
+            quantise_h(c, 0)
             times_window(c, 1)
-            held = B2 and c + 1 == last
-            for jt in range(T):
-                if not (held and jt == 1):
-                    exponent(c + 1, jt)
-                if not (held and jt >= 1):
-                    gauss(c + 1, jt)
-            if c == 0:
-                for r in range(EARLY4, 2):
-                    scale(8 + r, 1, "S")
-            if c > 0:
-                sum_squares(c - 1)
-            quant_h(c, 1)
-            quant_z(c + 1, 0)
-            quant_z(c + 1, 1)
-            first_g = T if (B2 and c + 1 == last) else 0
-            second_mm(c, 0)
-            if held:
-                exponent(last, 1)
-                for jt in range(1, T):
-                    gauss(last, jt)
-            second_mm(c, 1)
-            first_mm(c + 1, first_g)
-            first_mm(c + 1, first_g + 1)
-            for k, level, engines in W1[c + 1]:
-                if level == 0:
-                    make_factor(k, level)
-                for r in range(2):
-                    if engines[r] == "G":
-                        scale(2 * k + r, level, "G")
-            if B2 and c + 1 == last:
-                gabor(last, 0)
-                for jt in (T, T + 1):
-                    exponent(last, jt)
-                    gauss(last, jt)
-            for n in range(2):
-                add_b2(c, n)
-                first_mm(c + 1, first_g + n + 2)
-            if B2 and c + 1 == last:
-                for jt in (T + 2, T + 3):
-                    exponent(last, jt)
-                    gauss(last, jt)
-            for n in range(2):
-                maps(c, n)
-            for k, level, engines in W1[c + 1]:
-                for r in range(2):
-                    if engines[r] == "S":
-                        scale(2 * k + r, level, "S")
-            if c == 1:
-                scale(15, 1, "S")
-
-        c = last
-        if B2:
-            for jt in range(T, JT):
-                times_wave(c, jt)
-                if jt < T + 2:
-                    second_mm(c - 1, jt - 2)
-            for jt in range(NB, T):
-                first_mm(c, jt)
-            for n in range(2, TPC):
-                add_b2(c - 1, n)
-                if MAPS_FIRST:
-                    maps(c - 1, n)
-            for jt in range(NB):
-                first_mm(c, jt, "s")
-                add_b1(c, jt)
-            for jt in range(NB, T):
-                times_wave(c, jt)
-            for n in range(2, TPC):
-                if not MAPS_FIRST:
-                    maps(c - 1, n)
-            store_maps(c - 1)
-            square(c - 1)
-            times_window(c, 1)
-            if SUM_EARLY:
-                sum_squares(c - 1)
-            quant_h(c, 1)
-            for n in range(TPC):
-                second_pass(c, n, 1)
-            times_window(c, 0)
-            if not SUM_EARLY:
-                sum_squares(c - 1)
-            for cc in range(last):
-                inv_norm(cc)
-            if SUM_EARLY:
-                normals(0, nc.vector)
-            quant_h(c, 0)
-            for n in range(TPC):
-                second_pass(c, n, 0)
-            if not SUM_EARLY:
-                normals(0, nc.vector)
-            else:
-                normals(1, nc.vector)
-        else:
-            for jt in range(T):
-                times_wave(c, jt)
-                if jt < 2:
-                    second_mm(c - 1, jt + 2)
-                else:
-                    first_mm(c, jt + 2)
-            for n in range(2, TPC):
-                add_b2(c - 1, n)
-                maps(c - 1, n)
-                first_mm(c, n + T)
-            store_maps(c - 1)
-            square(c - 1)
-            gauss4(c, 1)
-            times_window(c, 0)
-            for jt in range(T, JT):
-                times_wave(c, jt)
-                if jt == T + 1:
+            if c + 1 < LAST:
+                windows(c + 1, range(SLOTS))
+                if c > 0:
+                    scale(ahead + TPC, 1, on_scalar=True)
                     sum_squares(c - 1)
-                    for cc in range(last):
-                        inv_norm(cc)
-            quant_h(c, 0)
-            times_window(c, 1)
-            normals(0, nc.vector)
-            quant_h(c, 1)
-            normals(1, nc.vector)
-        for n in range(TPC):
-            add_b2(c, n, slice(2 * PL, C) if TAILSPLIT else slice(0, C))
+                scale(ahead + TPC + 1, 1, on_scalar=True)
+                quantise_h(c, 1)
+                quantise_z(c + 1)
+                second_matmul(c, 0)
+                second_matmul(c, 1)
+                first_matmul(c + 1, 0)
+                first_matmul(c + 1, 1)
+                more_to_come = c + 2 < LAST
+                make_one_minus(ahead + TPC + 2, 2 if more_to_come else 1)
+                scale(ahead + TPC + 2, 0)
+                scale(ahead + TPC + 3, 0 if more_to_come else 1)
+                scale(ahead + TPC + 2, 1)
+                for n in range(2):
+                    add_b2(c, n)
+                    first_matmul(c + 1, n + 2)
+                for n in range(2):
+                    maps(c, n)
+                if more_to_come:
+                    scale(ahead + TPC + 3, 1, on_scalar=True)
+
+        c = LAST - 1
+        windows(LAST, [0])
+        exponent(LAST, 2)
+        exponent(LAST, 3)
+        sum_squares(c - 1)
+        quantise_h(c, 1)
+        quantise_z(LAST)
+        second_matmul(c, 0)
+        exponent(LAST, 1)
+        for jt in range(1, SLOTS):
+            gauss(LAST, jt)
+        second_matmul(c, 1)
+        first_matmul(LAST, SLOTS)
+        first_matmul(LAST, SLOTS + 1)
+        wave_into_window(LAST, 0)
+        windows(LAST, [SLOTS, SLOTS + 1])
+        for n in range(2):
+            add_b2(c, n)
+            first_matmul(LAST, SLOTS + 2 + n)
+        windows(LAST, [SLOTS + 2, SLOTS + 3])
+        for n in range(2):
             maps(c, n)
+        for jt in range(SLOTS, JT):
+            times_wave(LAST, jt)
+            if jt < SLOTS + 2:
+                second_matmul(c, jt - 2)
+        for n in range(2, TPC):
+            add_b2(c, n)
+        for jt in range(SLOTS):
+            first_matmul(LAST, jt, "s")
+            add_b1(LAST, jt)
+        for n in range(2, TPC):
+            maps(c, n)
+        store_maps(c, 0, TPC)
+        square(c)
+        times_window(LAST, 1)
+        quantise_h(LAST, 1)
+        for n in range(TPC):
+            second_pass(LAST, n, 1)
+        times_window(LAST, 0)
+        sum_squares(c)
+        for done in range(LAST):
+            inverse_root(done)
+        quantise_h(LAST, 0)
+        for n in range(TPC):
+            second_pass(LAST, n, 0)
+        normals(0)
+        for n in range(TPC):
+            add_b2(LAST, n)
+            maps(LAST, n)
             if n > 0:
-                store_maps(c, 0 if n == 1 else n, n + 1)
-        if TAILSPLIT:
-            for n in range(TPC):
-                add_b2(c, n, slice(0, 2 * PL))
-        if not SUM_EARLY:
-            normals(1, nc.vector)
-        square(last)
-        normals(last - 1, nc.vector)
-        sum_squares(last)
-        inv_norm(last)
-        normals(last, nc.vector)
+                store_maps(LAST, 0 if n == 1 else n, n + 1)
+        normals(1)
+        square(LAST)
+        normals(2)
+        sum_squares(LAST)
+        inverse_root(LAST)
+        normals(LAST)

@@ -28,11 +28,15 @@ CHUNKS = TILES // TPC
 LAST = CHUNKS - 1
 NORMAL = 2 * PLANE
 PARAM_ROW = 16
+FEATURE_ROW = 8
 FEATURES = 6
 
 PE_SINE_STEPS = 3
 BLEND_FIRST, BLEND_EVERY = 5, 2
+SPREAD_STEP = 2
 SCALAR_SHARE = 4
+MIP_BUFS = 4
+ARG_BUFS = 3
 SCALED_BUFS = 6
 
 
@@ -57,20 +61,17 @@ def tile_gabor_texture_decoder_f7_kernel(
             return psum.tile(shape, dtype, name=ring, tag=ring)
 
         s1_raw = work.tile([P, GROUPS, N], U8, name="s1_raw", tag="window", align_bytes=64)
-        features_t = work.tile([P, TILES, P], BF16, name="features_t", tag="h_in", align_bytes=64)
-        om_rows = const("om_rows", [P, N], BF16)
+        features_t = const("features_t", [P, TILES + P // FEATURE_ROW - 1, FEATURE_ROW], BF16)
+        features_flat = features_t[:].rearrange("p n f -> p (n f)")
+        om_rows = const("om_rows", [P, GROUP], BF16)
         mu_rows = const("mu_rows", [P, N], BF16)
-        s2 = const("s2", [P, GROUPS, C], U8)
-        nc.vector.memset(features_t[:].bitcast(I32), 0)
-        nc.vector.memset(om_rows[:].bitcast(I32), 0)
-        nc.vector.memset(s1_raw[:].bitcast(I32), 0)
-        nc.vector.memset(mu_rows[:].bitcast(I32), 0)
-        nc.vector.memset(s2[:].bitcast(I32), 0)
-        nc.vector.memset(mu_rows[0:FEATURES, :], -0.5)
         ident_b = const("ident_b", [P, P], BF16)
         make_identity(nc, ident_b[:])
-        ident = const("ident", [P, P], F32)
-        make_identity(nc, ident[:])
+        nc.vector.memset(features_flat.bitcast(I32), 0)
+        nc.vector.memset(mu_rows[:].bitcast(I32), 0)
+        nc.vector.memset(om_rows[:].bitcast(I32), 0)
+        nc.vector.memset(mu_rows[0:FEATURES, :], -0.5)
+        nc.vector.memset(s1_raw[:].bitcast(I32), 0)
 
         def load_by_j(name, vec, rows):
             dst = const(name, [P, rows * GROUPS, PARAM_ROW], BF16)[:, :, 0:SLOTS]
@@ -89,7 +90,7 @@ def tile_gabor_texture_decoder_f7_kernel(
 
         def load_mips(pair):
             for level in range(2):
-                m = work.tile([P, 2, L], BF16, name="mip%d" % level, tag="mip%d" % level, bufs=4)
+                m = work.tile([P, 2, L], BF16, name="mip%d" % level, tag="mip%d" % level, bufs=MIP_BUFS)
                 nc.sync.dma_start(out=m[:], in_=mip_hbm[level][:, 2 * pair : 2 * (pair + 1), :])
                 mips[2 * pair, level], mips[2 * pair + 1, level] = m[:, 0, :], m[:, 1, :]
 
@@ -99,25 +100,22 @@ def tile_gabor_texture_decoder_f7_kernel(
         phi_j = load_by_j("phi_j", phi, 1)
         frac_sb = const("frac_sb", [P, TILES], BF16)
         nc.sync.dma_start(out=frac_sb[:], in_=frac.rearrange("(p n) -> p n", n=TILES))
-        for pair in range(3):
+        for pair in range(MIP_BUFS - 1):
             load_mips(pair)
         w1_raw = work.tile([P, GROUPS, 2 * N], U8, name="w1_raw", tag="window", align_bytes=64)
         nc.sync.dma_start(out=w1_raw[:].bitcast(I32), in_=w1_words.rearrange("g p b -> p g b").bitcast(I32))
         load_scales(s1_raw, w1_scales)
-        nc.sync.dma_start(out=om_rows[0:2, :], in_=omega)
+        nc.sync.dma_start(out=om_rows[0:2, :], in_=omega[:, N - GROUP : N])
         mu_j = load_by_j("mu_j", mu, 2)
         gamma_j = load_by_j("gamma_j", gamma, 1)
         b1_j = load_by_j("b1_j", b1, 1)
         nc.sync.dma_start(out=mu_rows[0:2, :], in_=mu)
-        load_mips(3)
+        load_mips(MIP_BUFS - 1)
         w2 = const("w2", [P, GROUPS, C], U32)
         nc.sync.dma_start(out=w2[:].bitcast(I32), in_=w2_words.rearrange("g p n t -> p g (n t)").bitcast(I32))
-        load_scales(s2, w2_scales)
+        s2 = const("s2", [P, GROUPS, C], U8)
         b2_bc = const("b2_bc", [P, C], BF16)
         nc.sync.dma_start(out=b2_bc[:], in_=b2.partition_broadcast(P))
-
-        warm = const("warm", [P, 1], F32)
-        nc.scalar.activation(out=warm[:], in_=ident_b[:, 0:1], func=ACT.Sin)
 
         def by_group(table):
             return table[:].rearrange("p (g t) -> p g t", t=SLOTS)
@@ -131,17 +129,21 @@ def tile_gabor_texture_decoder_f7_kernel(
         om0_inv = const("om0_inv", [P, JT], F32)
         ratio = const("ratio", [P, JT], F32)
         phi_f = const("phi_f", [P, JT], F32)
+        ident = const("ident", [P, P], F32)
         nc.vector.tensor_tensor(out=uv_sq[:], in0=uv3, in1=uv3, op=ALU.mult)
         nc.vector.tensor_tensor(out=by_group(om_sq), in0=om_u, in1=om_u, op=ALU.mult)
-        nc.vector.tensor_copy(out=features_t[:, :, 0:2], in_=uv3)
+        nc.vector.tensor_copy(out=features_t[:, 0:TILES, 0:2], in_=uv3)
         nc.vector.tensor_scalar(
             out=om_shift[:], in0=om_sq[:], scalar1=2.0**-80, scalar2=2.0**-39, op0=ALU.is_lt, op1=ALU.mult
         )
-        nc.vector.tensor_copy(out=features_t[:, :, 2:4], in_=uv_sq[:])
+        nc.vector.tensor_copy(out=features_t[:, 0:TILES, 2:4], in_=uv_sq[:])
         nc.vector.tensor_tensor(out=by_group(om0), in0=om_u, in1=by_group(om_shift), op=ALU.add)
-        nc.vector.tensor_tensor(out=features_t[:, :, 4:6], in0=uv_sq[:], in1=features_t[:, :, 2:4], op=ALU.subtract)
+        nc.vector.tensor_tensor(
+            out=features_t[:, 0:TILES, 4:6], in0=uv_sq[:], in1=features_t[:, 0:TILES, 2:4], op=ALU.subtract
+        )
         nc.vector.reciprocal(out=om0_inv[:], in_=om0[:])
         nc.vector.tensor_copy(out=by_group(phi_f), in_=phi_j)
+        nc.vector.tensor_copy(out=ident[:], in_=ident_b[:])
         nc.vector.tensor_tensor(out=by_group(ratio), in0=om_v, in1=by_group(om0_inv), op=ALU.mult)
 
         gamma_f = const("gamma_f", [P, JT], F32)
@@ -195,19 +197,17 @@ def tile_gabor_texture_decoder_f7_kernel(
         def feature_rows(half):
             b = bank("s", [P, 2 * CHUNK], BF16)
             for n in range(2 * TPC):
-                nc.tensor.transpose(b[:, P * n : P * (n + 1)], features_t[:, 2 * TPC * half + n, :], ident_b[:])
+                first = FEATURE_ROW * (2 * TPC * half + n)
+                nc.tensor.transpose(b[:, P * n : P * (n + 1)], features_flat[:, first : first + P], ident_b[:])
             rows = const("features%d" % half, [P, 2 * CHUNK], BF16)
             nc.scalar.copy(out=rows[:], in_=b[:])
             features[2 * half], features[2 * half + 1] = rows[:, 0:CHUNK], rows[:, CHUNK : 2 * CHUNK]
 
-        def columns_of(rows, jt):
-            g, t = divmod(jt, SLOTS)
-            return rows[:, GROUP * g + t : GROUP * (g + 1) : SLOTS]
 
         def sine_by_vector(half, jt):
             g, t = divmod(jt, SLOTS)
             col = slice(jt, jt + 1)
-            arg = work.tile([P, 2, CHUNK], F32, name="arg", tag="arg", bufs=3)
+            arg = work.tile([P, 2, CHUNK], F32, name="arg", tag="arg", bufs=ARG_BUFS)
             nc.vector.scalar_tensor_tensor(
                 out=arg[:].rearrange("p c i -> p (c i)"), in0=v_rows[half][:], scalar=ratio[:, col],
                 in1=u_bank[half][:], op0=ALU.mult, op1=ALU.add,
@@ -220,7 +220,7 @@ def tile_gabor_texture_decoder_f7_kernel(
             g, t = divmod(jt, SLOTS)
             for c in (2 * half, 2 * half + 1):
                 b = bank("s", [P, CHUNK], F32)
-                nc.tensor.matmul(out=b[:], lhsT=columns_of(om_rows, jt), rhs=features[c], start=True, stop=True)
+                nc.tensor.matmul(out=b[:], lhsT=om_rows[:, t:GROUP:SLOTS], rhs=features[c], start=True, stop=True)
                 nc.scalar.activation(out=hidden[c, g][:, t, :], in_=b[:], func=ACT.Sin, bias=phi_f[:, jt : jt + 1])
 
         frac_f = const("frac_f", [P, TILES], F32)
@@ -234,12 +234,14 @@ def tile_gabor_texture_decoder_f7_kernel(
             for r in range(count):
                 one_minus[first + r] = o[:, r : r + 1]
 
-        def scale(tile, level, on_scalar=False):
+        def scale(tile, level, engine="gpsimd"):
             s = work.tile([P, GROUPS, SLOTS, P], F32, name="scaled%d" % level, tag="scaled%d" % level, bufs=SCALED_BUFS)
             src = mips[tile, level].rearrange("p (g m t) -> p g t m", g=GROUPS, t=SLOTS)
             factor = one_minus[tile] if level == 0 else frac_f[:, tile : tile + 1]
-            if on_scalar:
+            if engine == "scalar":
                 nc.scalar.activation(out=s[:], in_=src, func=ACT.Copy, scale=factor)
+            elif engine == "vector":
+                nc.vector.tensor_scalar(out=s[:], in0=src, scalar1=factor, scalar2=None, op0=ALU.mult)
             else:
                 nc.gpsimd.tensor_scalar(out=s[:], in0=src, scalar1=factor, scalar2=0.0, op0=ALU.mult, op1=ALU.add)
             scaled[tile, level] = s
@@ -274,7 +276,8 @@ def tile_gabor_texture_decoder_f7_kernel(
         def quantise(src, tag, bufs):
             codes = work.tile([P, CHUNK], U32, name=tag, tag=tag, bufs=bufs, align_bytes=64)
             scales = work.tile([P, CHUNK], U8, name=tag + "_s", tag=tag + "_s", bufs=bufs, align_bytes=64)
-            nc.vector.quantize_mx(out=codes[:].bitcast(FP8X4), scales=scales[:], in_=src[:].rearrange("p i t -> p (i t)"))
+            values = src[:].rearrange("p i t -> p (i t)")
+            nc.vector.quantize_mx(out=codes[:].bitcast(FP8X4), scales=scales[:], in_=values)
             return codes, scales
 
         def quantise_z(c):
@@ -301,8 +304,10 @@ def tile_gabor_texture_decoder_f7_kernel(
             )
 
         def exponent(c, jt):
+            g, t = divmod(jt, SLOTS)
             b = bank("s", [P, CHUNK], F32)
-            nc.tensor.matmul(out=b[:], lhsT=columns_of(mu_rows, jt), rhs=features[c], start=True, stop=True)
+            columns = mu_rows[:, GROUP * g + t : GROUP * (g + 1) : SLOTS]
+            nc.tensor.matmul(out=b[:], lhsT=columns, rhs=features[c], start=True, stop=True)
             e_bank[c, jt] = b
 
         def gauss(c, jt):
@@ -402,6 +407,7 @@ def tile_gabor_texture_decoder_f7_kernel(
             half, jt = divmod(step, JT)
             if step == steps - PE_SINE_STEPS:
                 sort_w1()
+                scale(SCALED_BUFS + 1, 1, "vector")
             if step < steps - PE_SINE_STEPS:
                 sine_by_vector(half, jt)
             else:
@@ -410,7 +416,7 @@ def tile_gabor_texture_decoder_f7_kernel(
                 for tile in range(SCALED_BUFS):
                     scale(tile, 0)
                     scale(tile, 1)
-            if step == 2:
+            if step == SPREAD_STEP:
                 spread_uv(1)
             if step in blend_steps:
                 n = blend_steps.index(step)
@@ -419,18 +425,19 @@ def tile_gabor_texture_decoder_f7_kernel(
                     round_z(n, g)
                 if n == 1:
                     scale(SCALED_BUFS, 1)
-                    scale(SCALED_BUFS + 1, 1)
                 if n % 2 == 1:
-                    load_mips(4 + n // 2)
+                    load_mips(MIP_BUFS + n // 2)
             if step - 1 in blend_steps[0::2]:
                 feature_rows(1 - blend_steps.index(step - 1) // 2)
         quantise_z(0)
+        nc.vector.memset(s2[:].bitcast(I32), 0)
+        load_scales(s2, w2_scales)
         window_tables()
         windows(0, range(SLOTS))
         make_one_minus(TPC + 2, 2)
         scale(TPC + 2, 0)
         scale(TPC + 3, 0)
-        scale(2 * TPC, 1, on_scalar=True)
+        scale(2 * TPC, 1, "scalar")
         for jt in range(SLOTS):
             first_matmul(0, jt)
 
@@ -456,7 +463,6 @@ def tile_gabor_texture_decoder_f7_kernel(
             if c + 1 < LAST:
                 make_one_minus(ahead + TPC, 2)
                 scale(ahead + TPC, 0)
-                scale(ahead + TPC + 1, 0)
             else:
                 make_one_minus(TILES - 1, 1)
                 scale(TILES - 1, 0)
@@ -467,16 +473,17 @@ def tile_gabor_texture_decoder_f7_kernel(
             blend_pair(ahead + 2, 0)
             blend_pair(ahead + 2, 1)
             if c == 0:
-                load_mips(6)
-                load_mips(7)
+                for pair in range(MIP_BUFS + 2, TILES // 2):
+                    load_mips(pair)
             quantise_h(c, 0)
             times_window(c, 1)
             if c + 1 < LAST:
+                scale(ahead + TPC + 1, 0, "vector")
                 windows(c + 1, range(SLOTS))
                 if c > 0:
-                    scale(ahead + TPC, 1, on_scalar=True)
+                    scale(ahead + TPC, 1, "scalar")
                     sum_squares(c - 1)
-                scale(ahead + TPC + 1, 1, on_scalar=True)
+                scale(ahead + TPC + 1, 1, "scalar")
                 quantise_h(c, 1)
                 quantise_z(c + 1)
                 second_matmul(c, 0)
@@ -494,7 +501,7 @@ def tile_gabor_texture_decoder_f7_kernel(
                 for n in range(2):
                     maps(c, n)
                 if more_to_come:
-                    scale(ahead + TPC + 3, 1, on_scalar=True)
+                    scale(ahead + TPC + 3, 1, "scalar")
 
         c = LAST - 1
         windows(LAST, [0])
@@ -550,7 +557,7 @@ def tile_gabor_texture_decoder_f7_kernel(
                 store_maps(LAST, 0 if n == 1 else n, n + 1)
         normals(1)
         square(LAST)
-        normals(2)
+        normals(LAST - 1)
         sum_squares(LAST)
         inverse_root(LAST)
         normals(LAST)

from contextlib import ExitStack

import concourse.mybir as mybir
from concourse.masks import make_identity

M, L, N, C, PLANE = 2048, 1024, 1024, 512, 64
FLOPS = 2 * M * L * N + 2 * M * N * C

F32 = mybir.dt.float32
BF16 = mybir.dt.bfloat16
U32 = mybir.dt.uint32
I32 = mybir.dt.int32
U8 = mybir.dt.uint8
FP8X4 = mybir.dt.float8_e4m3fn_x4
FP4X4 = mybir.dt.float4_e2m1fn_x4
ALU = mybir.AluOpType
ACT = mybir.ActivationFunctionType

P = 128
SLOTS = 4
GROUP = P * SLOTS
GROUPS = L // GROUP
JT = GROUPS * SLOTS
TILES = M // P
TPC = 4
CHUNK = TPC * P
CHUNKS = TILES // TPC
LAST = CHUNKS - 1
NORMAL = 2 * PLANE
PARAM_ROW = 16
FEATURE_ROW = 8
FEATURES = 6

PE_SINE_STEPS = 3
BLEND_FIRST, BLEND_EVERY = 5, 2
SPREAD_STEP = 2
SCALAR_SHARE = 4
MIP_BUFS = 4
ARG_BUFS = 3
SCALED_BUFS = 6


def tile_gabor_texture_decoder_f7_kernel(
    tc, mip0, mip1, frac, uv, w1_words, w1_scales, b1, omega, phi, mu, gamma, w2_words, w2_scales, b2, out_0, out_1
):
    nc = tc.nc
    mip_hbm = [m.rearrange("(p n) l -> p n l", n=TILES) for m in (mip0, mip1)]
    normal_hbm = out_0.rearrange("(p n) c -> p n c", n=TILES)
    maps_hbm = out_1.rearrange("(p n) c -> p n c", n=TILES)

    with ExitStack() as ctx:
        keep = ctx.enter_context(tc.tile_pool(name="keep", bufs=1))
        work = ctx.enter_context(tc.tile_pool(name="work", bufs=2))
        psum = ctx.enter_context(tc.psum_pool(name="psum", bufs=4))
        ctx.enter_context(tc.manual_schedule())

        def const(name, shape, dtype):
            return keep.tile(shape, dtype, name=name, align_bytes=64)

        def bank(ring, shape, dtype):
            return psum.tile(shape, dtype, name=ring, tag=ring)

        s1_raw = work.tile([P, GROUPS, N], U8, name="s1_raw", tag="window", align_bytes=64)
        features_t = const("features_t", [P, TILES + P // FEATURE_ROW - 1, FEATURE_ROW], BF16)
        features_flat = features_t[:].rearrange("p n f -> p (n f)")
        om_rows = const("om_rows", [P, GROUP], BF16)
        mu_rows = const("mu_rows", [P, N], BF16)
        ident_b = const("ident_b", [P, P], BF16)
        make_identity(nc, ident_b[:])
        nc.vector.memset(features_flat.bitcast(I32), 0)
        nc.vector.memset(mu_rows[:].bitcast(I32), 0)
        nc.vector.memset(om_rows[:].bitcast(I32), 0)
        nc.vector.memset(mu_rows[0:FEATURES, :], -0.5)
        nc.vector.memset(s1_raw[:].bitcast(I32), 0)

        def load_by_j(name, vec, rows):
            dst = const(name, [P, rows * GROUPS, PARAM_ROW], BF16)[:, :, 0:SLOTS]
            form = "d (g p t) -> p (d g) t" if rows > 1 else "(g p t) -> p g t"
            nc.sync.dma_start(out=dst, in_=vec.rearrange(form, p=P, t=SLOTS))
            return dst

        def load_scales(plane, scales):
            for q in range(4):
                nc.sync.dma_start(
                    out=plane[32 * q : 32 * q + 4, :, :].bitcast(I32),
                    in_=scales[:, 4 * q : 4 * q + 4, :].rearrange("g r n -> r g n").bitcast(I32),
                )

        mips = {}

        def load_mips(pair):
            for level in range(2):
                m = work.tile([P, 2, L], BF16, name="mip%d" % level, tag="mip%d" % level, bufs=MIP_BUFS)
                nc.sync.dma_start(out=m[:], in_=mip_hbm[level][:, 2 * pair : 2 * (pair + 1), :])
                mips[2 * pair, level], mips[2 * pair + 1, level] = m[:, 0, :], m[:, 1, :]

        uv_sb = const("uv_sb", [P, TILES * 2], BF16)
        nc.sync.dma_start(out=uv_sb[:], in_=uv.rearrange("(p n) d -> p (n d)", n=TILES))
        om_j = load_by_j("om_j", omega, 2)
        phi_j = load_by_j("phi_j", phi, 1)
        frac_sb = const("frac_sb", [P, TILES], BF16)
        nc.sync.dma_start(out=frac_sb[:], in_=frac.rearrange("(p n) -> p n", n=TILES))
        for pair in range(MIP_BUFS - 1):
            load_mips(pair)
        w1_raw = work.tile([P, GROUPS, 2 * N], U8, name="w1_raw", tag="window", align_bytes=64)
        nc.sync.dma_start(out=w1_raw[:].bitcast(I32), in_=w1_words.rearrange("g p b -> p g b").bitcast(I32))
        load_scales(s1_raw, w1_scales)
        nc.sync.dma_start(out=om_rows[0:2, :], in_=omega[:, N - GROUP : N])
        mu_j = load_by_j("mu_j", mu, 2)
        gamma_j = load_by_j("gamma_j", gamma, 1)
        b1_j = load_by_j("b1_j", b1, 1)
        nc.sync.dma_start(out=mu_rows[0:2, :], in_=mu)
        load_mips(MIP_BUFS - 1)
        w2 = const("w2", [P, GROUPS, C], U32)
        nc.sync.dma_start(out=w2[:].bitcast(I32), in_=w2_words.rearrange("g p n t -> p g (n t)").bitcast(I32))
        s2 = const("s2", [P, GROUPS, C], U8)
        b2_bc = const("b2_bc", [P, C], BF16)
        nc.sync.dma_start(out=b2_bc[:], in_=b2.partition_broadcast(P))

        def by_group(table):
            return table[:].rearrange("p (g t) -> p g t", t=SLOTS)

        uv3 = uv_sb[:].rearrange("p (n d) -> p n d", d=2)
        om_u, om_v = om_j[:, 0:GROUPS, :], om_j[:, GROUPS : 2 * GROUPS, :]
        uv_sq = const("uv_sq", [P, TILES, 2], F32)
        om_sq = const("om_sq", [P, JT], F32)
        om_shift = const("om_shift", [P, JT], F32)
        om0 = const("om0", [P, JT], F32)
        om0_inv = const("om0_inv", [P, JT], F32)
        ratio = const("ratio", [P, JT], F32)
        phi_f = const("phi_f", [P, JT], F32)
        ident = const("ident", [P, P], F32)
        nc.vector.tensor_tensor(out=uv_sq[:], in0=uv3, in1=uv3, op=ALU.mult)
        nc.vector.tensor_tensor(out=by_group(om_sq), in0=om_u, in1=om_u, op=ALU.mult)
        nc.vector.tensor_copy(out=features_t[:, 0:TILES, 0:2], in_=uv3)
        nc.vector.tensor_scalar(
            out=om_shift[:], in0=om_sq[:], scalar1=2.0**-80, scalar2=2.0**-39, op0=ALU.is_lt, op1=ALU.mult
        )
        nc.vector.tensor_copy(out=features_t[:, 0:TILES, 2:4], in_=uv_sq[:])
        nc.vector.tensor_tensor(out=by_group(om0), in0=om_u, in1=by_group(om_shift), op=ALU.add)
        nc.vector.tensor_tensor(
            out=features_t[:, 0:TILES, 4:6], in0=uv_sq[:], in1=features_t[:, 0:TILES, 2:4], op=ALU.subtract
        )
        nc.vector.reciprocal(out=om0_inv[:], in_=om0[:])
        nc.vector.tensor_copy(out=by_group(phi_f), in_=phi_j)
        nc.vector.tensor_copy(out=ident[:], in_=ident_b[:])
        nc.vector.tensor_tensor(out=by_group(ratio), in0=om_v, in1=by_group(om0_inv), op=ALU.mult)

        gamma_f = const("gamma_f", [P, JT], F32)
        b1_f = const("b1_f", [P, JT], F32)
        window_bias = const("window_bias", [P, JT], F32)

        def window_tables():
            mu_sq = const("mu_sq", [P, 2 * JT], F32)
            mu_norm = const("mu_norm", [P, JT], F32)
            nc.vector.tensor_copy(out=by_group(gamma_f), in_=gamma_j)
            nc.vector.tensor_tensor(out=by_group(mu_sq), in0=mu_j, in1=mu_j, op=ALU.mult)
            nc.vector.tensor_copy(out=by_group(b1_f), in_=b1_j)
            nc.vector.tensor_tensor(out=mu_norm[:], in0=mu_sq[:, 0:JT], in1=mu_sq[:, JT : 2 * JT], op=ALU.add)
            nc.vector.scalar_tensor_tensor(
                out=window_bias[:], in0=mu_norm[:], scalar=-0.5, in1=gamma_f[:], op0=ALU.mult, op1=ALU.mult
            )

        w1 = const("w1", [P, GROUPS * JT, 2 * P], U8)
        s1 = const("s1", [P, GROUPS * JT, P], U8)

        def sort_w1():
            nc.vector.tensor_copy(
                out=w1[:].rearrange("p (a t) (m b) -> p a t m b", t=SLOTS, b=2),
                in_=w1_raw[:].rearrange("p g (h m t b) -> p (g h) t m b", h=GROUPS, t=SLOTS, b=2),
            )
            nc.vector.tensor_copy(
                out=s1[:].rearrange("p (a t) m -> p a t m", t=SLOTS),
                in_=s1_raw[:].rearrange("p g (h m t) -> p (g h) t m", h=GROUPS, t=SLOTS),
            )

        hidden, hidden_half, u_bank, v_rows, features = {}, {}, {}, {}, {}
        for half in range(2):
            for g in range(GROUPS):
                both = const("hidden%d_%d" % (half, g), [P, 2, SLOTS, CHUNK], F32)
                hidden_half[half, g] = both
                hidden[2 * half, g], hidden[2 * half + 1, g] = both[:, 0], both[:, 1]

        def spread(half, d, ring):
            b = bank(ring, [P, 2 * CHUNK], BF16)
            for n in range(2 * TPC):
                col = 2 * (2 * TPC * half + n) + d
                nc.tensor.transpose(b[:, P * n : P * (n + 1)], uv_sb[:, col : col + 1].to_broadcast([P, P]), ident_b[:])
            return b

        def spread_uv(half):
            v_bank = spread(half, 1, "s")
            u_bank[half] = spread(half, 0, "v")
            v_rows[half] = work.tile([P, 2 * CHUNK], BF16, name="v_rows", tag="v_rows")
            nc.scalar.copy(out=v_rows[half][:], in_=v_bank[:])

        def feature_rows(half):
            b = bank("s", [P, 2 * CHUNK], BF16)
            for n in range(2 * TPC):
                first = FEATURE_ROW * (2 * TPC * half + n)
                nc.tensor.transpose(b[:, P * n : P * (n + 1)], features_flat[:, first : first + P], ident_b[:])
            rows = const("features%d" % half, [P, 2 * CHUNK], BF16)
            nc.scalar.copy(out=rows[:], in_=b[:])
            features[2 * half], features[2 * half + 1] = rows[:, 0:CHUNK], rows[:, CHUNK : 2 * CHUNK]


        def sine_by_vector(half, jt):
            g, t = divmod(jt, SLOTS)
            col = slice(jt, jt + 1)
            arg = work.tile([P, 2, CHUNK], F32, name="arg", tag="arg", bufs=ARG_BUFS)
            nc.vector.scalar_tensor_tensor(
                out=arg[:].rearrange("p c i -> p (c i)"), in0=v_rows[half][:], scalar=ratio[:, col],
                in1=u_bank[half][:], op0=ALU.mult, op1=ALU.add,
            )
            nc.scalar.activation(
                out=hidden_half[half, g][:, :, t, :], in_=arg[:], func=ACT.Sin, bias=phi_f[:, col], scale=om0[:, col]
            )

        def sine_by_matmul(half, jt):
            g, t = divmod(jt, SLOTS)
            for c in (2 * half, 2 * half + 1):
                b = bank("s", [P, CHUNK], F32)
                nc.tensor.matmul(out=b[:], lhsT=om_rows[:, t:GROUP:SLOTS], rhs=features[c], start=True, stop=True)
                nc.scalar.activation(out=hidden[c, g][:, t, :], in_=b[:], func=ACT.Sin, bias=phi_f[:, jt : jt + 1])

        frac_f = const("frac_f", [P, TILES], F32)
        one_minus, scaled, z_bank, z_in, z_q = {}, {}, {}, {}, {}

        def make_one_minus(first, count):
            o = const("one_minus%d" % first, [P, count], F32)
            nc.vector.tensor_scalar(
                out=o[:], in0=frac_sb[:, first : first + count], scalar1=-1.0, scalar2=1.0, op0=ALU.mult, op1=ALU.add
            )
            for r in range(count):
                one_minus[first + r] = o[:, r : r + 1]

        def scale(tile, level, engine="gpsimd"):
            s = work.tile([P, GROUPS, SLOTS, P], F32, name="scaled%d" % level, tag="scaled%d" % level, bufs=SCALED_BUFS)
            src = mips[tile, level].rearrange("p (g m t) -> p g t m", g=GROUPS, t=SLOTS)
            factor = one_minus[tile] if level == 0 else frac_f[:, tile : tile + 1]
            if engine == "scalar":
                nc.scalar.activation(out=s[:], in_=src, func=ACT.Copy, scale=factor)
            elif engine == "vector":
                nc.vector.tensor_scalar(out=s[:], in0=src, scalar1=factor, scalar2=None, op0=ALU.mult)
            else:
                nc.gpsimd.tensor_scalar(out=s[:], in0=src, scalar1=factor, scalar2=0.0, op0=ALU.mult, op1=ALU.add)
            scaled[tile, level] = s

        def blend(tile, g):
            b = bank("s", [P, SLOTS, P], F32)
            for t in range(SLOTS):
                for level in range(2):
                    nc.tensor.matmul(
                        out=b[:, t, :], lhsT=scaled[tile, level][:, g, t, :], rhs=ident[:],
                        is_transpose=True, start=(level == 0), stop=(level == 1),
                    )
            z_bank[tile, g] = b

        def round_z(tile, g):
            c, n = divmod(tile, TPC)
            if (c, g) not in z_in:
                z_in[c, g] = work.tile([P, CHUNK, SLOTS], BF16, name="z_in", tag="z_in", align_bytes=64)
            dst = z_in[c, g][:, P * n : P * (n + 1), :]
            src = z_bank[tile, g][:].rearrange("p t i -> p i t")
            if c == 0 and (GROUPS * n + g) % SCALAR_SHARE != 0:
                nc.vector.tensor_copy(out=dst, in_=src)
            else:
                nc.scalar.copy(out=dst, in_=src)

        def blend_pair(first, g):
            for tile in (first, first + 1):
                blend(tile, g)
            for tile in (first, first + 1):
                round_z(tile, g)

        def quantise(src, tag, bufs):
            codes = work.tile([P, CHUNK], U32, name=tag, tag=tag, bufs=bufs, align_bytes=64)
            scales = work.tile([P, CHUNK], U8, name=tag + "_s", tag=tag + "_s", bufs=bufs, align_bytes=64)
            values = src[:].rearrange("p i t -> p (i t)")
            nc.vector.quantize_mx(out=codes[:].bitcast(FP8X4), scales=scales[:], in_=values)
            return codes, scales

        def quantise_z(c):
            for g in range(GROUPS):
                z_q[c, g] = quantise(z_in[c, g], "z_q", 2 * GROUPS)

        a_bank, e_bank, window, h_in, h_q = {}, {}, {}, {}, {}

        def first_matmul(c, jt, ring="v"):
            b = bank(ring, [P, CHUNK], F32)
            for g in range(GROUPS):
                nc.tensor.matmul_mx(
                    out=b[:], lhsT=w1[:, g * JT + jt, :].bitcast(FP4X4), lhsT_scale=s1[:, g * JT + jt, :],
                    rhs=z_q[c, g][0][:].bitcast(FP8X4), rhs_scale=z_q[c, g][1][:],
                    start=(g == 0), stop=(g == GROUPS - 1),
                )
            a_bank[c, jt] = b

        def times_wave(c, jt):
            g, t = divmod(jt, SLOTS)
            w = hidden[c, g][:, t, :]
            nc.vector.scalar_tensor_tensor(
                out=w, in0=a_bank[c, jt][:], scalar=b1_f[:, jt : jt + 1], in1=w, op0=ALU.add, op1=ALU.mult
            )

        def exponent(c, jt):
            g, t = divmod(jt, SLOTS)
            b = bank("s", [P, CHUNK], F32)
            columns = mu_rows[:, GROUP * g + t : GROUP * (g + 1) : SLOTS]
            nc.tensor.matmul(out=b[:], lhsT=columns, rhs=features[c], start=True, stop=True)
            e_bank[c, jt] = b

        def gauss(c, jt):
            g, t = divmod(jt, SLOTS)
            if (c, g) not in window:
                window[c, g] = work.tile([P, SLOTS, CHUNK], F32, name="window", tag="window", align_bytes=64)
            col = slice(jt, jt + 1)
            nc.scalar.activation(
                out=window[c, g][:, t, :], in_=e_bank[c, jt][:], func=ACT.Exp,
                bias=window_bias[:, col], scale=gamma_f[:, col],
            )

        def windows(c, jts):
            for jt in jts:
                exponent(c, jt)
                gauss(c, jt)

        def wave_into_window(c, g):
            for t in range(0, SLOTS, 2):
                w = window[c, g][:, t : t + 2, :]
                nc.gpsimd.tensor_tensor(out=w, in0=w, in1=hidden[c, g][:, t : t + 2, :], op=ALU.mult)

        def add_b1(c, jt):
            g, t = divmod(jt, SLOTS)
            nc.scalar.activation(
                out=hidden[c, g][:, t, :], in_=a_bank[c, jt][:], func=ACT.Identity, bias=b1_f[:, jt : jt + 1]
            )

        def times_window(c, g):
            h = work.tile([P, CHUNK, SLOTS], BF16, name="h_in", tag="h_in", align_bytes=64)
            nc.vector.tensor_tensor(
                out=h[:].rearrange("p (i e) t -> p i t e", e=2),
                in0=hidden[c, g].rearrange("p t (i e) -> p i t e", e=2),
                in1=window[c, g][:].rearrange("p t (i e) -> p i t e", e=2),
                op=ALU.mult,
            )
            h_in[c, g] = h

        def quantise_h(c, g):
            h_q[c, g] = quantise(h_in[c, g], "h_q", GROUPS)

        y_bank, squares, norm = {}, {}, {}

        def second_pass(c, n, g):
            opens = (c, n) not in y_bank
            if opens:
                y_bank[c, n] = bank("v", [P, C], F32)
            cols = slice(P * n, P * (n + 1))
            nc.tensor.matmul_mx(
                out=y_bank[c, n][:], lhsT=h_q[c, g][0][:, cols].bitcast(FP8X4), lhsT_scale=h_q[c, g][1][:, cols],
                rhs=w2[:, g, :].bitcast(FP8X4), rhs_scale=s2[:, g, :], start=opens, stop=not opens,
            )

        def second_matmul(c, n):
            for g in range(GROUPS):
                second_pass(c, n, g)

        def add_b2(c, n):
            nc.vector.tensor_tensor(out=hidden[c, 0][:, n, :], in0=y_bank[c, n][:], in1=b2_bc[:], op=ALU.add)

        def maps(c, n):
            v = hidden[c, 0][:, n, NORMAL:C]
            nc.scalar.activation(out=v, in_=v, func=ACT.Tanh)

        def store_maps(c, n0, n1):
            nc.sync.dma_start(out=maps_hbm[:, TPC * c + n0 : TPC * c + n1, :], in_=hidden[c, 0][:, n0:n1, NORMAL:C])

        def square(c):
            squares[c] = work.tile([P, TPC, NORMAL], F32, name="squares", tag="squares", bufs=1)
            v = hidden[c, 0][:, :, 0:NORMAL]
            if c < LAST:
                nc.scalar.activation(out=squares[c][:], in_=v, func=ACT.Square)
            else:
                nc.vector.tensor_tensor(out=squares[c][:], in0=v, in1=v, op=ALU.mult)

        def sum_squares(c):
            norm[c] = const("norm%d" % c, [P, TPC, PLANE], F32)
            nc.vector.tensor_tensor(
                out=norm[c][:], in0=squares[c][:, :, 0:PLANE], in1=squares[c][:, :, PLANE:NORMAL], op=ALU.add
            )

        def inverse_root(c):
            nc.scalar.activation(out=norm[c][:], in_=norm[c][:], func=ACT.Abs_reciprocal_sqrt, bias=1.0)

        def normals(c):
            v = hidden[c, 0][:, :, 0:NORMAL].rearrange("p n (h x) -> p n h x", h=2)
            r = norm[c][:].unsqueeze(2).to_broadcast([P, TPC, 2, PLANE])
            nc.vector.tensor_tensor(out=v, in0=v, in1=r, op=ALU.mult)
            nc.sync.dma_start(out=normal_hbm[:, TPC * c : TPC * (c + 1), :], in_=hidden[c, 0][:, :, 0:NORMAL])

        make_one_minus(0, SCALED_BUFS)
        nc.vector.tensor_copy(out=frac_f[:], in_=frac_sb[:])
        spread_uv(0)
        steps = 2 * JT
        blend_steps = [BLEND_FIRST + BLEND_EVERY * n for n in range(TPC)]
        for step in range(steps):
            half, jt = divmod(step, JT)
            if step == steps - PE_SINE_STEPS:
                sort_w1()
                scale(SCALED_BUFS + 1, 1, "vector")
            if step < steps - PE_SINE_STEPS:
                sine_by_vector(half, jt)
            else:
                sine_by_matmul(half, jt)
            if step == 0:
                for tile in range(SCALED_BUFS):
                    scale(tile, 0)
                    scale(tile, 1)
            if step == SPREAD_STEP:
                spread_uv(1)
            if step in blend_steps:
                n = blend_steps.index(step)
                for g in range(GROUPS):
                    blend(n, g)
                    round_z(n, g)
                if n == 1:
                    scale(SCALED_BUFS, 1)
                if n % 2 == 1:
                    load_mips(MIP_BUFS + n // 2)
            if step - 1 in blend_steps[0::2]:
                feature_rows(1 - blend_steps.index(step - 1) // 2)
        quantise_z(0)
        nc.vector.memset(s2[:].bitcast(I32), 0)
        load_scales(s2, w2_scales)
        window_tables()
        windows(0, range(SLOTS))
        make_one_minus(TPC + 2, 2)
        scale(TPC + 2, 0)
        scale(TPC + 3, 0)
        scale(2 * TPC, 1, "scalar")
        for jt in range(SLOTS):
            first_matmul(0, jt)

        for c in range(LAST):
            ahead = TPC * (c + 1)
            for jt in range(SLOTS):
                times_wave(c, jt)
                if c == 0:
                    first_matmul(c, jt + SLOTS)
                elif jt < 2:
                    second_matmul(c - 1, jt + 2)
                else:
                    first_matmul(c, jt + 2)
            if c > 0:
                for n in range(2, TPC):
                    add_b2(c - 1, n)
                    maps(c - 1, n)
                    first_matmul(c, n + SLOTS)
                store_maps(c - 1, 0, TPC)
                square(c - 1)
            windows(c, range(SLOTS, JT))
            times_window(c, 0)
            if c + 1 < LAST:
                make_one_minus(ahead + TPC, 2)
                scale(ahead + TPC, 0)
            else:
                make_one_minus(TILES - 1, 1)
                scale(TILES - 1, 0)
            blend_pair(ahead, 0)
            for jt in range(SLOTS, JT):
                times_wave(c, jt)
            blend_pair(ahead, 1)
            blend_pair(ahead + 2, 0)
            blend_pair(ahead + 2, 1)
            if c == 0:
                for pair in range(MIP_BUFS + 2, TILES // 2):
                    load_mips(pair)
            quantise_h(c, 0)
            times_window(c, 1)
            if c + 1 < LAST:
                scale(ahead + TPC + 1, 0, "vector")
                windows(c + 1, range(SLOTS))
                if c > 0:
                    scale(ahead + TPC, 1, "scalar")
                    sum_squares(c - 1)
                scale(ahead + TPC + 1, 1, "scalar")
                quantise_h(c, 1)
                quantise_z(c + 1)
                second_matmul(c, 0)
                second_matmul(c, 1)
                first_matmul(c + 1, 0)
                first_matmul(c + 1, 1)
                more_to_come = c + 2 < LAST
                make_one_minus(ahead + TPC + 2, 2 if more_to_come else 1)
                scale(ahead + TPC + 2, 0)
                scale(ahead + TPC + 3, 0 if more_to_come else 1)
                scale(ahead + TPC + 2, 1)
                for n in range(2):
                    add_b2(c, n)
                    first_matmul(c + 1, n + 2)
                for n in range(2):
                    maps(c, n)
                if more_to_come:
                    scale(ahead + TPC + 3, 1, "scalar")

        c = LAST - 1
        windows(LAST, [0])
        exponent(LAST, 2)
        exponent(LAST, 3)
        sum_squares(c - 1)
        quantise_h(c, 1)
        quantise_z(LAST)
        second_matmul(c, 0)
        exponent(LAST, 1)
        for jt in range(1, SLOTS):
            gauss(LAST, jt)
        second_matmul(c, 1)
        first_matmul(LAST, SLOTS)
        first_matmul(LAST, SLOTS + 1)
        wave_into_window(LAST, 0)
        windows(LAST, [SLOTS, SLOTS + 1])
        for n in range(2):
            add_b2(c, n)
            first_matmul(LAST, SLOTS + 2 + n)
        windows(LAST, [SLOTS + 2, SLOTS + 3])
        for n in range(2):
            maps(c, n)
        for jt in range(SLOTS, JT):
            times_wave(LAST, jt)
            if jt < SLOTS + 2:
                second_matmul(c, jt - 2)
        for n in range(2, TPC):
            add_b2(c, n)
        for jt in range(SLOTS):
            first_matmul(LAST, jt, "s")
            add_b1(LAST, jt)
        for n in range(2, TPC):
            maps(c, n)
        store_maps(c, 0, TPC)
        square(c)
        times_window(LAST, 1)
        quantise_h(LAST, 1)
        for n in range(TPC):
            second_pass(LAST, n, 1)
        times_window(LAST, 0)
        sum_squares(c)
        for done in range(LAST):
            inverse_root(done)
        quantise_h(LAST, 0)
        for n in range(TPC):
            second_pass(LAST, n, 0)
        normals(0)
        for n in range(TPC):
            add_b2(LAST, n)
            maps(LAST, n)
            if n > 0:
                store_maps(LAST, 0 if n == 1 else n, n + 1)
        normals(1)
        square(LAST)
        normals(LAST - 1)
        sum_squares(LAST)
        inverse_root(LAST)
        normals(LAST)
